import numpy as np, ml_dtypes
CORES = [14,30,46,142,158,174,270,286,302,398,414,430]
N = 12
PG, W, NP = 32, 64, 32
CAPP = 8
def entries(a): return a.T.reshape(-1)
def pack(v, P): return np.ascontiguousarray(np.asarray(v, np.int32).reshape(-1, P).T)
def lists(rng, how):
    I = rng.integers(0, N * PG, (N, NP))
    if how == "alike": I[:] = rng.integers(0, N * PG, (N, 1))
    if how == "hotrank": I = PG * int(rng.integers(N)) + rng.integers(0, PG, (N, NP))
    if how == "own": I = PG * np.arange(N).reshape(N, 1) + rng.integers(0, PG, (N, NP))
    if how == "edge": I = PG * rng.integers(0, N, (N, NP)) + np.where(rng.random((N, NP)) < 0.5, 0, PG - 1)
    if how == "swap": s = int(rng.integers(1, N)); I = np.stack([PG * ((r + s) % N) + np.concatenate([rng.permutation(PG), rng.integers(0, PG, NP)])[:NP] for r in range(N)])
    O = np.stack([rng.permutation(np.repeat(rng.permutation(N)[:NP // CAPP], CAPP)) if how == "full" else rng.permutation(np.repeat(np.arange(N), CAPP))[:NP] for r in range(N)])
    I = PG * O + I % PG
    if how == "full": I = PG * O + np.stack([np.array([np.sum(O[r, :i] == O[r, i]) for i in range(NP)]) for r in range(N)]) % PG
    if how == "sorted": I = np.sort(I, axis=1)
    return {"pt": np.stack([pack(I[r], 16) for r in range(N)])}
def setup_inputs(rng):
    return dict({"pool": rng.standard_normal((N, PG * 128, W), dtype=np.float32).astype(ml_dtypes.bfloat16)}, **lists(rng, "uniform"))
def setup_inputs_alike(rng):
    d = setup_inputs(rng); d.update(lists(rng, "alike"))
    for k in ("pool",): d[k] = (d[k].astype(np.float32) * 1048576.0).astype(d[k].dtype)
    return d
def setup_inputs_edge(rng):
    d = setup_inputs(rng); d.update(lists(rng, "edge"))
    for k in ("pool",): d[k] = (d[k].astype(np.float32) * (1 / 1024.0)).astype(d[k].dtype)
    return d
def setup_inputs_full(rng):
    d = setup_inputs(rng); d.update(lists(rng, "full"))
    return d
def setup_inputs_sorted(rng):
    d = setup_inputs(rng); d.update(lists(rng, "sorted"))
    return d
def check_inputs(x):
    bad = []
    if x["pt"].min() < 0 or x["pt"].max() >= N * PG: bad.append("pt out of range")
    if max(int(np.bincount(entries(a) // PG, minlength=N).max()) for a in x["pt"]) > CAPP: bad.append("more than CAPP entries of a list point into one rank's part")
    return bad
def reference(pool, pt):
    A = np.concatenate(list(pool), axis=0).reshape(N * PG, 128, W)
    return {"y": np.stack([A[entries(pt[r])].reshape(NP * 128, W) for r in range(N)])}

@@ -1,0 +1,303 @@
+from concourse.bass import DstId, RemoteDMATransfer, IndirectOffsetOnAxis
+from concourse.mybir import dt, AluOpType, AxisListType
+
+N, PG, NP, CAPP = 12, 32, 32, 8
+SUB = 16
+RW = 512
+BLK = CAPP * SUB
+
+SCRATCH = {
+    "ptd": ("dram", [128, 2], "int32"),
+    "inbox": ("dram", [3, 128, 2], "int32"),
+    "tab": ("dram", [PG * SUB, RW], "bfloat16"),
+    "land": ("dram", [N * BLK, RW], "bfloat16"),
+    "zero": ("sbuf", [128, 224], "int32"),
+    "sb": ("sbuf", [128, 3 * RW], "bfloat16"),
+    "fin": ("sbuf", [128, 4 * RW], "bfloat16"),
+    "lcol": ("sbuf", [128, 8], "int32"),
+    "own": ("sbuf", [128, 8], "int32"),
+    "e": ("sbuf", [128, 8], "float32"),
+    "vv": ("sbuf", [128, 8], "float32"),
+    "w": ("sbuf", [128, 8], "float32"),
+    "idx": ("sbuf", [128, 8], "int32"),
+    "A": ("sbuf", [128, 3 * 128], "float32"),
+    "ones": ("sbuf", [128, 32], "float32"),
+    "U": ("sbuf", [128, 32], "float32"),
+    "iotaK": ("sbuf", [128, 128], "float32"),
+    "pidx": ("sbuf", [128, 4], "int32"),
+    "pq": ("sbuf", [128, 4], "int32"),
+    "qc": ("sbuf", [128, 4], "float32"),
+    "ownr": ("sbuf", [128, 4], "int32"),
+    "ownf": ("sbuf", [128, 4], "float32"),
+    "own128": ("sbuf", [128, 4], "float32"),
+    "iotaO": ("sbuf", [128, 12], "float32"),
+    "OH": ("sbuf", [128, 12], "float32"),
+    "Pm": ("sbuf", [128, 12], "float32"),
+    "kk": ("sbuf", [128, 4], "float32"),
+    "sv": ("sbuf", [128, 4], "float32"),
+    "J": ("sbuf", [128, 512], "float32"),
+    "Sel": ("sbuf", [128, 512], "float32"),
+    "fidx": ("sbuf", [128, 4], "int32"),
+    "pk": ("psum", [128, 512], "float32"),
+    "pi": ("psum", [128, 512], "float32"),
+    "pkd": ("psum", [128, 512], "float32"),
+    "pid": ("psum", [128, 512], "float32"),
+    "pc": ("psum", [128, 512], "float32"),
+    "pf": ("psum", [128, 512], "float32"),
+}
+SEMAPHORES = ["ptc", "tabc", "lq", "rq", "lqd", "rep", "ld", "ldd", "ldr", "vs", "ts", "gi", "gj",
+              "gs0", "gs1", "gs2", "darr", "arr", "snt", "selfc", "fg0", "fg1", "fg2", "fg3", "st"]
+
+_PLAN = {}
+
+
+def _chip_cores(c, topo):
+    n = topo.CORES_PER_CHIP
+    return [x for x in range(max(0, c - n), c + n) if topo.host(x) == topo.host(c) and topo.chip(x) == topo.chip(c)]
+
+
+def make_plan(cores, topo):
+    side = {}
+    for R in cores:
+        cc = _chip_cores(R, topo)
+        pairs = [cc[i:i + 2] for i in range(0, len(cc), 2)]
+        others = [p for p in pairs if R not in p]
+        others.sort(key=lambda p: topo.die(p[0]) == topo.die(R))
+        side[R] = others
+    chips = sorted(set(topo.chip(R) for R in cores))
+    nch = len(chips)
+    roles = {}
+    for o, R in enumerate(cores):
+        roles[R] = {"kind": "rank", "o": o, "jobs": {}, "helpers": [p[0] for p in side[R]], "direct": [], "relays": []}
+        for p in side[R]:
+            roles[p[0]] = {"kind": "helper", "o": o, "jobs": {}}
+    for o, Ro in enumerate(cores):
+        hA, hB, hC = [p[0] for p in side[Ro]]
+        mates6 = [x for x in cores if topo.rack(topo.host(x)) == topo.rack(topo.host(Ro))]
+        for r, Rr in enumerate(cores):
+            if r == o:
+                continue
+            rel3 = (chips.index(topo.chip(Rr)) - chips.index(topo.chip(Ro))) % nch
+            if not topo.may_write(Ro, Rr):
+                X = [x for x in cores if topo.chip(x) == topo.chip(Ro) and topo.may_write(Ro, x)
+                     and topo.rack(topo.host(x)) == topo.rack(topo.host(Rr))][0]
+                srv, rel = side[Ro][rel3][0], side[X][rel3][1]
+                roles[srv]["jobs"][2] = (r, rel)
+                roles[rel] = {"kind": "relay", "o": o, "r": r, "srv": srv}
+                roles[Rr]["relays"].append(rel)
+                continue
+            if topo.rack(topo.host(Ro)) != topo.rack(topo.host(Rr)):
+                srv, slot = [(hA, 0), (hC, 0), (Ro, 0)][rel3]
+            else:
+                rel6 = (mates6.index(Rr) - mates6.index(Ro)) % len(mates6)
+                srv, slot = [None, (hA, 1), (hB, 0), (hB, 1), (hC, 1), (Ro, 1)][rel6]
+            roles[srv]["jobs"][slot] = (r, None)
+            roles[Rr]["direct"].append((srv, slot))
+    return roles
+
+
+def rank_program(g, core, T, topo):
+    if "p" not in _PLAN:
+        _PLAN["p"] = make_plan(list(T.cores), topo)
+    role = _PLAN["p"].get(core)
+    if role is None:
+        return
+    S = T.sem
+    cores = list(T.cores)
+    v, te, sy, sc = g.vector, g.tensor, g.sync, g.scalar
+    cnt = {"vs": 0, "ts": 0, "snt": 0}
+    A = AluOpType
+
+    def engines(dsts):
+        m = topo.mask(core, dsts[0])
+        for d in dsts[1:]:
+            m &= topo.mask(core, d)
+        return [b for b in range(m.bit_length()) if (m >> b) & 1]
+
+    def bits(lst):
+        return sum(1 << b for b in lst)
+
+    def did(d):
+        rid, pid = topo.addr(d, core)
+        return DstId(rid=rid, pnc=pid)
+
+    def send(out_ap, in_ap, dst, sem, eng):
+        rid, pid = topo.addr(dst, core)
+        g.remote_dma(out_ap=out_ap, in_ap=in_ap, remote_sem=sem, local_sem=S.snt, pid=pid, routing_id=rid,
+                     dma_engine_mask=bits(eng))
+        cnt["snt"] += len(eng)
+
+    if role["kind"] == "relay":
+        srv, Rr, o = role["srv"], cores[role["r"]], role["o"]
+        g.wait_ge(S.rq, 1)
+        send(T.inbox[2], T.inbox[0], srv, S.lqd, engines([srv])[:1])
+        full = engines([Rr])
+        g.wait_ge(S.darr, len(engines([srv])))
+        send(T.land[BLK * o:BLK * (o + 1), :], T.land[0:BLK, :], Rr, S.arr, full)
+        g.wait_ge(S.snt, cnt["snt"])
+        return
+
+    is_rank = role["kind"] == "rank"
+    o = role["o"]
+    jobs = role["jobs"]
+
+    def V(make):
+        if cnt["vs"]:
+            v.wait_ge(S.vs, cnt["vs"])
+        make().then_inc(S.vs, 1)
+        cnt["vs"] += 1
+
+    def P(make):
+        make().then_inc(S.ts, 1)
+        cnt["ts"] += 1
+
+    if is_rank:
+        sy.dma_start(T.ptd[0:16, :], T.pt[:]).then_inc(S.ptc, 16)
+        V(lambda: v.memset(T.zero[0:1, 0:224], 0))
+        sc.wait_ge(S.vs, cnt["vs"])
+        sc.dma_start(T.ptd[16:128, :], T.zero[0:1, 0:224]).then_inc(S.ptc, 16)
+        sc.dma_start(T.lcol[0:32, 2:3], T.pt[:]).then_inc(S.ldr, 16)
+        sy.dma_start(T.tab[:], T.pool[:]).then_inc(S.tabc, 16)
+
+    V(lambda: v.memset(T.ones[0:32, 0:32], 1.0))
+    g.wait_ge(S.vs, cnt["vs"])
+    g.affine_select(T.U[0:32, 0:32], T.ones[0:32, 0:32], [[1, 32]], A.is_gt, 0.0, 0, -1).then_inc(S.gi, 1)
+    g.iota(T.iotaK[0:32, 0:128], [[1, CAPP], [0, SUB]], 0, 0, allow_small_or_imprecise_dtypes=True).then_inc(S.gi, 1)
+    g.iota(T.pidx[:, 0:1], [[1, 1]], 0, 1).then_inc(S.gi, 1)
+    ngi = 3
+    if is_rank:
+        g.iota(T.iotaO[0:32, 0:N], [[1, N]], 0, 0, allow_small_or_imprecise_dtypes=True).then_inc(S.gi, 1)
+        ngi = 4
+    v.wait_ge(S.gi, ngi)
+    te.wait_ge(S.gi, ngi)
+    V(lambda: v.tensor_scalar(T.pq[:, 0:1], T.pidx[:, 0:1], SUB - 1, None, A.bitwise_and))
+    V(lambda: v.tensor_copy(T.qc[:, 0:1], T.pq[:, 0:1]))
+
+    if is_rank:
+        g.wait_ge(S.ptc, 32)
+        rel, dr = role["relays"], role["direct"]
+        eng = engines(rel + [d for d, _ in dr])
+        g.remote_dma_fused([
+            RemoteDMATransfer(dst_ids=[did(d) for d in rel], dma_engine_mask=bits(eng[0:1]), remote_sem=S.rq,
+                              srcs=[T.ptd[:]], dsts=[T.inbox[0] for d in rel], alu_op=0),
+            RemoteDMATransfer(dst_ids=[did(d) for d, _ in dr], dma_engine_mask=bits(eng[1:2]), remote_sem=S.lq,
+                              srcs=[T.ptd[:]], dsts=[T.inbox[s] for _, s in dr], alu_op=0),
+        ], local_sem=S.snt)
+        cnt["snt"] += 2
+        g.wait_ge(S.tabc, 16)
+        hs = role["helpers"]
+        eng = engines(hs)
+        npc = (PG * SUB) // 128
+        per = len(eng) // npc
+        g.remote_dma_fused([
+            RemoteDMATransfer(dst_ids=[did(d) for d in hs], dma_engine_mask=bits(eng[i * per:(i + 1) * per]), remote_sem=S.rep,
+                              srcs=[T.tab[128 * i:128 * (i + 1), :]], dsts=[T.tab[128 * i:128 * (i + 1), :] for d in hs],
+                              alu_op=0)
+            for i in range(npc)], local_sem=S.snt)
+        cnt["snt"] += per * npc
+        for th in range(2):
+            g.iota(T.J[0:32, 256 * th:256 * (th + 1)], [[16, 2], [2, 8], [0, SUB]], th, -1,
+                   allow_small_or_imprecise_dtypes=True).then_inc(S.gj, 1)
+
+        v.wait_ge(S.ldr, 16)
+        V(lambda: v.tensor_scalar(T.ownr[0:32, 0:1], T.lcol[0:32, 2:3], 5, None, A.logical_shift_right))
+        V(lambda: v.tensor_copy(T.ownf[0:32, 0:1], T.ownr[0:32, 0:1]))
+        V(lambda: v.tensor_scalar(T.OH[0:32, 0:N], T.iotaO[0:32, 0:N], T.ownf[0:32, 0:1], None, A.is_equal))
+        te.wait_ge(S.vs, cnt["vs"])
+        P(lambda: te.matmul(T.pc[0:32, 0:N], T.U[0:32, 0:32], T.OH[0:32, 0:N], True, True))
+        V(lambda: v.tensor_scalar(T.own128[0:32, 0:1], T.ownf[0:32, 0:1], float(BLK), None, A.mult))
+        v.wait_ge(S.ts, cnt["ts"])
+        V(lambda: v.tensor_tensor(T.Pm[0:32, 0:N], T.pc[0:32, 0:N], T.OH[0:32, 0:N], A.mult))
+        V(lambda: v.tensor_reduce(T.kk[0:32, 0:1], T.Pm[0:32, 0:N], AxisListType.X, A.add))
+        V(lambda: v.tensor_scalar(T.sv[0:32, 0:1], T.kk[0:32, 0:1], float(SUB), T.own128[0:32, 0:1], A.mult, A.add))
+
+    def group(pairs_sc, pk, pi):
+        c0, c1 = pairs_sc[0][1], pairs_sc[-1][1] + 1
+        V(lambda: v.tensor_scalar(T.own[0:32, c0:c1], T.lcol[0:32, c0:c1], 5, None, A.logical_shift_right))
+        V(lambda: v.tensor_scalar(T.vv[0:32, c0:c1], T.lcol[0:32, c0:c1], float(PG * o), float(SUB), A.subtract, A.mult))
+        V(lambda: v.tensor_scalar(T.e[0:32, c0:c1], T.own[0:32, c0:c1], float(o), None, A.is_equal))
+        te.wait_ge(S.vs, cnt["vs"])
+        P(lambda: te.matmul(pk[0:32, c0:c1], T.U[0:32, 0:32], T.e[0:32, c0:c1], True, True))
+        V(lambda: v.tensor_tensor(T.w[0:32, c0:c1], T.vv[0:32, c0:c1], T.e[0:32, c0:c1], A.mult))
+        v.wait_ge(S.ts, cnt["ts"])
+        for s, c in pairs_sc:
+            V(lambda: v.tensor_scalar(T.A[0:32, 128 * s:128 * (s + 1)], T.iotaK[0:32, 0:128], pk[0:32, c:c + 1], None, A.is_equal))
+        te.wait_ge(S.vs, cnt["vs"])
+        for s, c in pairs_sc:
+            P(lambda: te.matmul(pi[:, c:c + 1], T.A[0:32, 128 * s:128 * (s + 1)], T.w[0:32, c:c + 1], True, True))
+        v.wait_ge(S.ts, cnt["ts"])
+        V(lambda: v.tensor_scalar(T.idx[:, c0:c1], pi[:, c0:c1], T.qc[:, 0:1], None, A.add))
+        return cnt["vs"]
+
+    def gather(s, c):
+        g.indirect_dma_start(T.sb[:, RW * s:RW * (s + 1)], None, T.tab[:],
+                             IndirectOffsetOnAxis(ap=T.idx[:, c:c + 1], axis=0),
+                             bounds_check=PG * SUB - 1).then_inc(S["gs%d" % s], 16)
+
+    def reply(s):
+        r, rel = jobs[s]
+        g.wait_ge(S["gs%d" % s], 16)
+        src = T.sb[:, RW * s:RW * (s + 1)]
+        if rel is None:
+            send(T.land[BLK * o:BLK * (o + 1), :], src, cores[r], S.arr, engines([cores[r]]))
+        else:
+            send(T.land[0:BLK, :], src, rel, S.darr, engines([rel]))
+
+    sy.wait_ge(S.lq, 2)
+    sy.dma_start(T.lcol[0:32, 0:1], T.inbox[0, 0:16, :]).then_inc(S.ld, 16)
+    sc.wait_ge(S.lq, 2)
+    sc.dma_start(T.lcol[0:32, 1:2], T.inbox[1, 0:16, :]).then_inc(S.ld, 16)
+    v.wait_ge(S.ld, 32)
+
+    if not is_rank:
+        n1 = group([(0, 0), (1, 1)], T.pk, T.pi)
+        sy.wait_ge(S.lqd, 1)
+        sy.dma_start(T.lcol[0:32, 4:5], T.inbox[2, 0:16, :]).then_inc(S.ldd, 16)
+        v.wait_ge(S.ldd, 16)
+        n2 = group([(2, 4)], T.pkd, T.pid)
+        g.wait_ge(S.rep, 16)
+        g.wait_ge(S.vs, n1)
+        gather(0, 0)
+        gather(1, 1)
+        g.wait_ge(S.vs, n2)
+        gather(2, 4)
+        reply(0)
+        reply(1)
+        reply(2)
+        g.wait_ge(S.snt, cnt["snt"])
+        return
+
+    n1 = group([(0, 0), (1, 1), (2, 2)], T.pk, T.pi)
+    v.wait_ge(S.gj, 2)
+    V(lambda: v.tensor_scalar(T.Sel[0:32, 0:512], T.J[0:32, 0:512], 0.0, None, A.is_equal))
+    te.wait_ge(S.vs, cnt["vs"])
+    for t in range(4):
+        P(lambda: te.matmul(T.pf[:, t:t + 1], T.Sel[0:32, 128 * t:128 * (t + 1)], T.sv[0:32, 0:1], True, True))
+    v.wait_ge(S.ts, cnt["ts"])
+    V(lambda: v.tensor_scalar(T.fidx[:, 0:4], T.pf[:, 0:4], T.qc[:, 0:1], None, A.add))
+    n2 = cnt["vs"]
+
+    g.wait_ge(S.vs, n1)
+    gather(0, 0)
+    gather(1, 1)
+    gather(2, 2)
+    reply(0)
+    reply(1)
+    sy.wait_ge(S.gs2, 16)
+    sy.dma_start(T.land[BLK * o:BLK * (o + 1), :], T.sb[:, RW * 2:RW * 3]).then_inc(S.selfc, 16)
+
+    narr = sum(len(engines([x])) for x in cores if x != core and topo.may_write(core, x))
+    narr += sum(len(engines([x])) for x in role["relays"])
+    g.wait_ge(S.arr, narr)
+    g.wait_ge(S.selfc, 16)
+    g.wait_ge(S.vs, n2)
+    for t in range(4):
+        g.indirect_dma_start(T.fin[:, RW * t:RW * (t + 1)], None, T.land[:],
+                             IndirectOffsetOnAxis(ap=T.fidx[:, t:t + 1], axis=0),
+                             bounds_check=N * BLK - 1).then_inc(S["fg%d" % t], 16)
+    for t in range(4):
+        q = sy if t % 2 == 0 else sc
+        q.wait_ge(S["fg%d" % t], 16)
+        q.dma_start(T.y[1024 * t:1024 * (t + 1), :], T.fin[:, RW * t:RW * (t + 1)]).then_inc(S.st, 16)
+    g.wait_ge(S.st, 64)
+    g.wait_ge(S.snt, cnt["snt"])

@@ -5,10 +5,11 @@ N, PG, NP, CAPP = 12, 32, 32, 8
 SUB = 16
 RW = 512
 BLK = CAPP * SUB
+NPC = (PG * SUB) // 128
 
 SCRATCH = {
     "ptd": ("dram", [128, 2], "int32"),
-    "inbox": ("dram", [3, 128, 2], "int32"),
+    "inbox": ("dram", [2, 128, 2], "int32"),
     "tab": ("dram", [PG * SUB, RW], "bfloat16"),
     "land": ("dram", [N * BLK, RW], "bfloat16"),
     "zero": ("sbuf", [128, 224], "int32"),
@@ -40,13 +41,11 @@ SCRATCH = {
     "fidx": ("sbuf", [128, 4], "int32"),
     "pk": ("psum", [128, 512], "float32"),
     "pi": ("psum", [128, 512], "float32"),
-    "pkd": ("psum", [128, 512], "float32"),
-    "pid": ("psum", [128, 512], "float32"),
     "pc": ("psum", [128, 512], "float32"),
     "pf": ("psum", [128, 512], "float32"),
 }
-SEMAPHORES = ["ptc", "tabc", "lq", "rq", "lqd", "rep", "ld", "ldd", "ldr", "vs", "ts", "gi", "gj",
-              "gs0", "gs1", "gs2", "darr", "arr", "snt", "selfc", "fg0", "fg1", "fg2", "fg3", "st"]
+SEMAPHORES = ["ptc", "tb0", "tb1", "tb2", "tb3", "lq", "pcs", "rep", "ld", "ldr", "vs", "ts", "gi", "gj",
+              "gs0", "gs1", "gs2", "arr", "snt", "selfc", "fg0", "fg1", "fg2", "fg3", "st"]
 
 _PLAN = {}
 
@@ -56,50 +55,58 @@ def _chip_cores(c, topo):
     return [x for x in range(max(0, c - n), c + n) if topo.host(x) == topo.host(c) and topo.chip(x) == topo.chip(c)]
 
 
+def _engines(m):
+    return [b for b in range(m.bit_length()) if (m >> b) & 1]
+
+
 def make_plan(cores, topo):
-    side = {}
-    for R in cores:
+    def rk(x):
+        return topo.rack(topo.host(x))
+
+    info = {}
+    for o, R in enumerate(cores):
         cc = _chip_cores(R, topo)
         pairs = [cc[i:i + 2] for i in range(0, len(cc), 2)]
         others = [p for p in pairs if R not in p]
         others.sort(key=lambda p: topo.die(p[0]) == topo.die(R))
-        side[R] = others
-    chips = sorted(set(topo.chip(R) for R in cores))
-    nch = len(chips)
+        partner = [x for x in cores if x != R and topo.chip(x) == topo.chip(R) and topo.may_write(R, x) and rk(x) != rk(R)][0]
+        mine = [x for p in pairs if R in p for x in p if x != R]
+        info[R] = (o, [p[0] for p in others], [p[1] for p in others] + mine, partner)
     roles = {}
-    for o, R in enumerate(cores):
-        roles[R] = {"kind": "rank", "o": o, "jobs": {}, "helpers": [p[0] for p in side[R]], "direct": [], "relays": []}
-        for p in side[R]:
-            roles[p[0]] = {"kind": "helper", "o": o, "jobs": {}}
-    for o, Ro in enumerate(cores):
-        hA, hB, hC = [p[0] for p in side[Ro]]
-        mates6 = [x for x in cores if topo.rack(topo.host(x)) == topo.rack(topo.host(Ro))]
-        for r, Rr in enumerate(cores):
-            if r == o:
-                continue
-            rel3 = (chips.index(topo.chip(Rr)) - chips.index(topo.chip(Ro))) % nch
-            if not topo.may_write(Ro, Rr):
-                X = [x for x in cores if topo.chip(x) == topo.chip(Ro) and topo.may_write(Ro, x)
-                     and topo.rack(topo.host(x)) == topo.rack(topo.host(Rr))][0]
-                srv, rel = side[Ro][rel3][0], side[X][rel3][1]
-                roles[srv]["jobs"][2] = (r, rel)
-                roles[rel] = {"kind": "relay", "o": o, "r": r, "srv": srv}
-                roles[Rr]["relays"].append(rel)
-                continue
-            if topo.rack(topo.host(Ro)) != topo.rack(topo.host(Rr)):
-                srv, slot = [(hA, 0), (hC, 0), (Ro, 0)][rel3]
-            else:
-                rel6 = (mates6.index(Rr) - mates6.index(Ro)) % len(mates6)
-                srv, slot = [None, (hA, 1), (hB, 0), (hB, 1), (hC, 1), (Ro, 1)][rel6]
-            roles[srv]["jobs"][slot] = (r, None)
-            roles[Rr]["direct"].append((srv, slot))
+    for R in cores:
+        o, home, prox, partner = info[R]
+        far = info[partner][2]
+        roles[R] = {"kind": "rank", "o": o, "jobs": {}, "home": home, "far": far, "servers": []}
+        for q, h in enumerate(home):
+            roles[h] = {"kind": "home", "o": o, "q": q, "jobs": {}, "home": [x for x in home if x != h], "far": far}
+        for q, p in enumerate(prox):
+            roles[p] = {"kind": "proxy", "o": info[partner][0], "q": q, "jobs": {}, "peers": [x for x in prox if x != p]}
+    for Ro in cores:
+        o, home, prox, partner = info[Ro]
+        far = info[partner][2]
+        near_t = [None, (Ro, 0), (Ro, 1), (home[0], 0), (home[1], 0), (home[2], 0)]
+        far_t = [(far[2], 0), (far[0], 0), (far[0], 1), (far[1], 0), (far[2], 1), (far[3], 0)]
+        for base, table in ((Ro, near_t), (partner, far_t)):
+            six = [x for x in cores if rk(x) == rk(base)]
+            for Rr in six:
+                t = table[(six.index(Rr) - six.index(base)) % len(six)]
+                if t is None:
+                    continue
+                roles[t[0]]["jobs"][t[1]] = cores.index(Rr)
+                roles[Rr]["servers"].append(t)
+    for c, role in roles.items():
+        m = -1
+        for s, r in role["jobs"].items():
+            m &= topo.mask(c, cores[r])
+        role["reng"] = _engines(m) if role["jobs"] else []
     return roles
 
 
 def rank_program(g, core, T, topo):
     if "p" not in _PLAN:
         _PLAN["p"] = make_plan(list(T.cores), topo)
-    role = _PLAN["p"].get(core)
+    plan = _PLAN["p"]
+    role = plan.get(core)
     if role is None:
         return
     S = T.sem
@@ -112,7 +119,7 @@ def rank_program(g, core, T, topo):
         m = topo.mask(core, dsts[0])
         for d in dsts[1:]:
             m &= topo.mask(core, d)
-        return [b for b in range(m.bit_length()) if (m >> b) & 1]
+        return _engines(m)
 
     def bits(lst):
         return sum(1 << b for b in lst)
@@ -127,17 +134,24 @@ def rank_program(g, core, T, topo):
                      dma_engine_mask=bits(eng))
         cnt["snt"] += len(eng)
 
-    if role["kind"] == "relay":
-        srv, Rr, o = role["srv"], cores[role["r"]], role["o"]
-        g.wait_ge(S.rq, 1)
-        send(T.inbox[2], T.inbox[0], srv, S.lqd, engines([srv])[:1])
-        full = engines([Rr])
-        g.wait_ge(S.darr, len(engines([srv])))
-        send(T.land[BLK * o:BLK * (o + 1), :], T.land[0:BLK, :], Rr, S.arr, full)
-        g.wait_ge(S.snt, cnt["snt"])
-        return
+    def piece(q):
+        return T.tab[128 * q:128 * (q + 1), :]
 
-    is_rank = role["kind"] == "rank"
+    def spread(q):
+        far, home = role["far"][q:q + 1], role["home"]
+        off = engines(far)
+        on = [b for b in engines(home) if b not in off]
+        g.remote_dma_fused([
+            RemoteDMATransfer(dst_ids=[did(d) for d in far], dma_engine_mask=bits(off), remote_sem=S.pcs,
+                              srcs=[piece(q)], dsts=[piece(q) for d in far], alu_op=0),
+            RemoteDMATransfer(dst_ids=[did(d) for d in home], dma_engine_mask=bits(on), remote_sem=S.rep,
+                              srcs=[piece(q)], dsts=[piece(q) for d in home], alu_op=0),
+        ], local_sem=S.snt)
+        cnt["snt"] += len(off) + len(on)
+        return len(off), len(on)
+
+    kind = role["kind"]
+    is_rank = kind == "rank"
     o = role["o"]
     jobs = role["jobs"]
 
@@ -157,7 +171,9 @@ def rank_program(g, core, T, topo):
         sc.wait_ge(S.vs, cnt["vs"])
         sc.dma_start(T.ptd[16:128, :], T.zero[0:1, 0:224]).then_inc(S.ptc, 16)
         sc.dma_start(T.lcol[0:32, 2:3], T.pt[:]).then_inc(S.ldr, 16)
-        sy.dma_start(T.tab[:], T.pool[:]).then_inc(S.tabc, 16)
+        rows = (PG * 128) // NPC
+        for q in range(NPC):
+            (sy if q % 2 == 0 else sc).dma_start(piece(q), T.pool[rows * q:rows * (q + 1), :]).then_inc(S["tb%d" % q], 16)
 
     V(lambda: v.memset(T.ones[0:32, 0:32], 1.0))
     g.wait_ge(S.vs, cnt["vs"])
@@ -173,28 +189,23 @@ def rank_program(g, core, T, topo):
     V(lambda: v.tensor_scalar(T.pq[:, 0:1], T.pidx[:, 0:1], SUB - 1, None, A.bitwise_and))
     V(lambda: v.tensor_copy(T.qc[:, 0:1], T.pq[:, 0:1]))
 
+    nrep = 0
     if is_rank:
         g.wait_ge(S.ptc, 32)
-        rel, dr = role["relays"], role["direct"]
-        eng = engines(rel + [d for d, _ in dr])
+        srv = role["servers"]
+        eng = engines([d for d, _ in srv])
+        half = (len(srv) + 1) // 2
         g.remote_dma_fused([
-            RemoteDMATransfer(dst_ids=[did(d) for d in rel], dma_engine_mask=bits(eng[0:1]), remote_sem=S.rq,
-                              srcs=[T.ptd[:]], dsts=[T.inbox[0] for d in rel], alu_op=0),
-            RemoteDMATransfer(dst_ids=[did(d) for d, _ in dr], dma_engine_mask=bits(eng[1:2]), remote_sem=S.lq,
-                              srcs=[T.ptd[:]], dsts=[T.inbox[s] for _, s in dr], alu_op=0),
-        ], local_sem=S.snt)
+            RemoteDMATransfer(dst_ids=[did(d) for d, _ in part], dma_engine_mask=bits(eng[i:i + 1]), remote_sem=S.lq,
+                              srcs=[T.ptd[:]], dsts=[T.inbox[s] for _, s in part], alu_op=0)
+            for i, part in enumerate((srv[:half], srv[half:]))], local_sem=S.snt)
         cnt["snt"] += 2
-        g.wait_ge(S.tabc, 16)
-        hs = role["helpers"]
-        eng = engines(hs)
-        npc = (PG * SUB) // 128
-        per = len(eng) // npc
-        g.remote_dma_fused([
-            RemoteDMATransfer(dst_ids=[did(d) for d in hs], dma_engine_mask=bits(eng[i * per:(i + 1) * per]), remote_sem=S.rep,
-                              srcs=[T.tab[128 * i:128 * (i + 1), :]], dsts=[T.tab[128 * i:128 * (i + 1), :] for d in hs],
-                              alu_op=0)
-            for i in range(npc)], local_sem=S.snt)
-        cnt["snt"] += per * npc
+        hs = role["home"]
+        for q, h in enumerate(hs):
+            g.wait_ge(S["tb%d" % q], 16)
+            send(piece(q), piece(q), h, S.pcs, engines([h]))
+        g.wait_ge(S["tb%d" % (NPC - 1)], 16)
+        spread(NPC - 1)
         for th in range(2):
             g.iota(T.J[0:32, 256 * th:256 * (th + 1)], [[16, 2], [2, 8], [0, SUB]], th, -1,
                    allow_small_or_imprecise_dtypes=True).then_inc(S.gj, 1)
@@ -210,6 +221,19 @@ def rank_program(g, core, T, topo):
         V(lambda: v.tensor_tensor(T.Pm[0:32, 0:N], T.pc[0:32, 0:N], T.OH[0:32, 0:N], A.mult))
         V(lambda: v.tensor_reduce(T.kk[0:32, 0:1], T.Pm[0:32, 0:N], AxisListType.X, A.add))
         V(lambda: v.tensor_scalar(T.sv[0:32, 0:1], T.kk[0:32, 0:1], float(SUB), T.own128[0:32, 0:1], A.mult, A.add))
+    elif kind == "home":
+        g.wait_ge(S.pcs, len(engines([cores[o]])))
+        noff, non = spread(role["q"])
+        nrep = non * (NPC - 1)
+    else:
+        g.wait_ge(S.pcs, len(engines([cores[o]])))
+        peers, q = role["peers"], role["q"]
+        eng = engines(peers)
+        g.remote_dma_fused([
+            RemoteDMATransfer(dst_ids=[did(d) for d in peers], dma_engine_mask=bits(eng), remote_sem=S.rep,
+                              srcs=[piece(q)], dsts=[piece(q) for d in peers], alu_op=0)], local_sem=S.snt)
+        cnt["snt"] += len(eng)
+        nrep = len(eng) * len(peers)
 
     def group(pairs_sc, pk, pi):
         c0, c1 = pairs_sc[0][1], pairs_sc[-1][1] + 1
@@ -235,35 +259,24 @@ def rank_program(g, core, T, topo):
                              bounds_check=PG * SUB - 1).then_inc(S["gs%d" % s], 16)
 
     def reply(s):
-        r, rel = jobs[s]
         g.wait_ge(S["gs%d" % s], 16)
-        src = T.sb[:, RW * s:RW * (s + 1)]
-        if rel is None:
-            send(T.land[BLK * o:BLK * (o + 1), :], src, cores[r], S.arr, engines([cores[r]]))
-        else:
-            send(T.land[0:BLK, :], src, rel, S.darr, engines([rel]))
+        send(T.land[BLK * o:BLK * (o + 1), :], T.sb[:, RW * s:RW * (s + 1)], cores[jobs[s]], S.arr, role["reng"])
 
-    sy.wait_ge(S.lq, 2)
-    sy.dma_start(T.lcol[0:32, 0:1], T.inbox[0, 0:16, :]).then_inc(S.ld, 16)
-    sc.wait_ge(S.lq, 2)
-    sc.dma_start(T.lcol[0:32, 1:2], T.inbox[1, 0:16, :]).then_inc(S.ld, 16)
-    v.wait_ge(S.ld, 32)
+    nj = len(jobs)
+    for s in range(nj):
+        q = sy if s % 2 == 0 else sc
+        q.wait_ge(S.lq, nj)
+        q.dma_start(T.lcol[0:32, s:s + 1], T.inbox[s, 0:16, :]).then_inc(S.ld, 16)
+    v.wait_ge(S.ld, 16 * nj)
 
     if not is_rank:
-        n1 = group([(0, 0), (1, 1)], T.pk, T.pi)
-        sy.wait_ge(S.lqd, 1)
-        sy.dma_start(T.lcol[0:32, 4:5], T.inbox[2, 0:16, :]).then_inc(S.ldd, 16)
-        v.wait_ge(S.ldd, 16)
-        n2 = group([(2, 4)], T.pkd, T.pid)
-        g.wait_ge(S.rep, 16)
+        n1 = group([(s, s) for s in range(nj)], T.pk, T.pi)
+        g.wait_ge(S.rep, nrep)
         g.wait_ge(S.vs, n1)
-        gather(0, 0)
-        gather(1, 1)
-        g.wait_ge(S.vs, n2)
-        gather(2, 4)
-        reply(0)
-        reply(1)
-        reply(2)
+        for s in range(nj):
+            gather(s, s)
+        for s in range(nj):
+            reply(s)
         g.wait_ge(S.snt, cnt["snt"])
         return
 
@@ -286,8 +299,7 @@ def rank_program(g, core, T, topo):
     sy.wait_ge(S.gs2, 16)
     sy.dma_start(T.land[BLK * o:BLK * (o + 1), :], T.sb[:, RW * 2:RW * 3]).then_inc(S.selfc, 16)
 
-    narr = sum(len(engines([x])) for x in cores if x != core and topo.may_write(core, x))
-    narr += sum(len(engines([x])) for x in role["relays"])
+    narr = sum(len(plan[d]["reng"]) for d, _ in role["servers"])
     g.wait_ge(S.arr, narr)
     g.wait_ge(S.selfc, 16)
     g.wait_ge(S.vs, n2)

@@ -1,51 +1,37 @@
 from concourse.bass import DstId, RemoteDMATransfer, IndirectOffsetOnAxis
 from concourse.mybir import dt, AluOpType, AxisListType
 
-N, PG, NP, CAPP = 12, 32, 32, 8
-SUB = 16
-RW = 512
-BLK = CAPP * SUB
-NPC = (PG * SUB) // 128
+N, PG, NP = 12, 32, 32
+QU = 4
+RW = 2048
+NH = 4
+PW = RW // NH
+NS = 16
+BW = RW // NS
+NB = NS // NH
+NR = 3
 
 SCRATCH = {
     "ptd": ("dram", [128, 2], "int32"),
-    "inbox": ("dram", [2, 128, 2], "int32"),
-    "tab": ("dram", [PG * SUB, RW], "bfloat16"),
-    "land": ("dram", [N * BLK, RW], "bfloat16"),
+    "inbox": ("dram", [NR, 128, 2], "int32"),
+    "tabs": ("dram", [N * PG * QU, BW], "bfloat16"),
+    "pcd": ("dram", [NB, 128, BW], "bfloat16"),
     "zero": ("sbuf", [128, 224], "int32"),
-    "sb": ("sbuf", [128, 3 * RW], "bfloat16"),
-    "fin": ("sbuf", [128, 4 * RW], "bfloat16"),
-    "lcol": ("sbuf", [128, 8], "int32"),
-    "own": ("sbuf", [128, 8], "int32"),
-    "e": ("sbuf", [128, 8], "float32"),
-    "vv": ("sbuf", [128, 8], "float32"),
-    "w": ("sbuf", [128, 8], "float32"),
-    "idx": ("sbuf", [128, 8], "int32"),
-    "A": ("sbuf", [128, 3 * 128], "float32"),
-    "ones": ("sbuf", [128, 32], "float32"),
-    "U": ("sbuf", [128, 32], "float32"),
-    "iotaK": ("sbuf", [128, 128], "float32"),
+    "P": ("sbuf", [128, RW], "bfloat16"),
+    "sb": ("sbuf", [128, NR * BW], "bfloat16"),
+    "fin": ("sbuf", [128, RW], "bfloat16"),
+    "lcol": ("sbuf", [128, 4], "int32"),
+    "val": ("sbuf", [128, 4], "float32"),
+    "idx": ("sbuf", [128, 4], "int32"),
     "pidx": ("sbuf", [128, 4], "int32"),
     "pq": ("sbuf", [128, 4], "int32"),
     "qc": ("sbuf", [128, 4], "float32"),
-    "ownr": ("sbuf", [128, 4], "int32"),
-    "ownf": ("sbuf", [128, 4], "float32"),
-    "own128": ("sbuf", [128, 4], "float32"),
-    "iotaO": ("sbuf", [128, 12], "float32"),
-    "OH": ("sbuf", [128, 12], "float32"),
-    "Pm": ("sbuf", [128, 12], "float32"),
-    "kk": ("sbuf", [128, 4], "float32"),
-    "sv": ("sbuf", [128, 4], "float32"),
-    "J": ("sbuf", [128, 512], "float32"),
-    "Sel": ("sbuf", [128, 512], "float32"),
-    "fidx": ("sbuf", [128, 4], "int32"),
-    "pk": ("psum", [128, 512], "float32"),
-    "pi": ("psum", [128, 512], "float32"),
-    "pc": ("psum", [128, 512], "float32"),
+    "J": ("sbuf", [128, 128], "float32"),
+    "Sel": ("sbuf", [128, 128], "float32"),
     "pf": ("psum", [128, 512], "float32"),
 }
-SEMAPHORES = ["ptc", "tb0", "tb1", "tb2", "tb3", "lq", "pcs", "rep", "ld", "ldr", "vs", "ts", "gi", "gj",
-              "gs0", "gs1", "gs2", "arr", "snt", "selfc", "fg0", "fg1", "fg2", "fg3", "st"]
+SEMAPHORES = ["ptc", "pl", "own", "lq", "pcs", "tbn", "tbf", "tb", "ld", "vs", "ts", "gi", "gs0", "gs1", "gs2",
+              "arr", "snt", "st"]
 
 _PLAN = {}
 
@@ -71,54 +57,74 @@ def make_plan(cores, topo):
         others.sort(key=lambda p: topo.die(p[0]) == topo.die(R))
         partner = [x for x in cores if x != R and topo.chip(x) == topo.chip(R) and topo.may_write(R, x) and rk(x) != rk(R)][0]
         mine = [x for p in pairs if R in p for x in p if x != R]
-        info[R] = (o, [p[0] for p in others], [p[1] for p in others] + mine, partner)
+        info[R] = (o, [p[0] for p in others] + [R], [p[1] for p in others] + mine, partner)
+    hosts = sorted({topo.host(R) for R in cores})
+    racks = sorted({topo.rack(h) for h in hosts})
+    taken = {(topo.host(R), topo.chip(R)) for R in cores}
+    dies = [topo.die(x) for x in info[cores[0]][1]]
+    per_die = max(dies.count(d) for d in dies) * NB
+    first, twin = {}, {}
+    for k in racks:
+        R0 = [R for R in cores if rk(R) == k][0]
+        cand = [x for x in range((max(hosts) + 1) * topo.CORES_PER_HOST)
+                if topo.same_plane(x, R0) and (topo.host(x), topo.chip(x)) not in taken]
+        hs = [h for h in hosts if topo.rack(h) == k]
+        places = []
+        for h in hs:
+            places += [(h, c) for c in sorted({topo.chip(x) for x in cand if topo.host(x) == h})[:per_die // len(hs)]]
+        seen = {}
+        first[k], twin[k] = [], []
+        for s in range(NS):
+            d = dies[s // NB]
+            i = seen.get(d, 0)
+            seen[d] = i + 1
+            two = [x for x in cand if (topo.host(x), topo.chip(x)) == places[i] and topo.die(x) == d][:2]
+            first[k].append(two[0])
+            twin[k].append(two[1])
+
+    def targets(c, q):
+        return [[first[rk(c)][NB * q + b]] for b in range(NB)]
+
     roles = {}
     for R in cores:
-        o, home, prox, partner = info[R]
+        o, hold, rel, partner = info[R]
         far = info[partner][2]
-        roles[R] = {"kind": "rank", "o": o, "jobs": {}, "home": home, "far": far, "servers": []}
-        for q, h in enumerate(home):
-            roles[h] = {"kind": "home", "o": o, "q": q, "jobs": {}, "home": [x for x in home if x != h], "far": far}
-        for q, p in enumerate(prox):
-            roles[p] = {"kind": "proxy", "o": info[partner][0], "q": q, "jobs": {}, "peers": [x for x in prox if x != p]}
-    for Ro in cores:
-        o, home, prox, partner = info[Ro]
-        far = info[partner][2]
-        near_t = [None, (Ro, 0), (Ro, 1), (home[0], 0), (home[1], 0), (home[2], 0)]
-        far_t = [(far[2], 0), (far[0], 0), (far[0], 1), (far[1], 0), (far[2], 1), (far[3], 0)]
-        for base, table in ((Ro, near_t), (partner, far_t)):
-            six = [x for x in cores if rk(x) == rk(base)]
-            for Rr in six:
-                t = table[(six.index(Rr) - six.index(base)) % len(six)]
-                if t is None:
-                    continue
-                roles[t[0]]["jobs"][t[1]] = cores.index(Rr)
-                roles[Rr]["servers"].append(t)
-    for c, role in roles.items():
-        m = -1
-        for s, r in role["jobs"].items():
-            m &= topo.mask(c, cores[r])
-        role["reng"] = _engines(m) if role["jobs"] else []
+        for q, c in enumerate(hold):
+            roles[c] = {"kind": "rank" if c == R else "hold", "o": o, "q": q, "relay": far[q], "to": targets(c, q), "src": R}
+        roles[R]["hold"] = hold[:-1]
+        hs = [h for h in hosts if topo.rack(h) == rk(R)]
+        roles[R]["srv"] = (first if topo.host(R) == hs[0] else twin)[rk(R)]
+        roles[R]["slot"] = [x for x in cores if topo.host(x) == topo.host(R)].index(R)
+        for q, c in enumerate(rel):
+            roles[c] = {"kind": "relay", "o": info[partner][0], "q": q, "to": targets(c, q), "src": info[partner][1][q]}
+    for k in racks:
+        hs = [h for h in hosts if topo.rack(h) == k]
+        near = [o for o, R in enumerate(cores) if rk(R) == k]
+        farp = [o for o, R in enumerate(cores) if rk(R) != k]
+        for s in range(NS):
+            roles[first[k][s]] = {"kind": "srv", "s": s, "reqs": [x for x in cores if topo.host(x) == hs[0]],
+                                  "twin": twin[k][s], "waves": [near, farp]}
+            roles[twin[k][s]] = {"kind": "srv", "s": s, "reqs": [x for x in cores if topo.host(x) == hs[1]],
+                                 "feeder": first[k][s], "waves": [near, farp]}
     return roles
 
 
 def rank_program(g, core, T, topo):
     if "p" not in _PLAN:
         _PLAN["p"] = make_plan(list(T.cores), topo)
-    plan = _PLAN["p"]
-    role = plan.get(core)
+    role = _PLAN["p"].get(core)
     if role is None:
         return
     S = T.sem
-    cores = list(T.cores)
     v, te, sy, sc = g.vector, g.tensor, g.sync, g.scalar
     cnt = {"vs": 0, "ts": 0, "snt": 0}
     A = AluOpType
+    kind = role["kind"]
 
-    def engines(dsts):
-        m = topo.mask(core, dsts[0])
-        for d in dsts[1:]:
-            m &= topo.mask(core, d)
+    def engines(src, dsts):
+        m = -1
+        for d in dsts:
+            m &= topo.mask(src, d)
         return _engines(m)
 
     def bits(lst):
@@ -128,32 +134,37 @@ def rank_program(g, core, T, topo):
         rid, pid = topo.addr(d, core)
         return DstId(rid=rid, pnc=pid)
 
-    def send(out_ap, in_ap, dst, sem, eng):
+    def send(out_ap, in_ap, dst, sem):
+        eng = engines(core, [dst])
         rid, pid = topo.addr(dst, core)
         g.remote_dma(out_ap=out_ap, in_ap=in_ap, remote_sem=sem, local_sem=S.snt, pid=pid, routing_id=rid,
                      dma_engine_mask=bits(eng))
         cnt["snt"] += len(eng)
 
-    def piece(q):
-        return T.tab[128 * q:128 * (q + 1), :]
+    def split(src, to):
+        eng = engines(src, [d for part in to for d in part])
+        w = 1
+        while 2 * w * len(to) <= len(eng):
+            w *= 2
+        return [eng[w * b:w * (b + 1)] for b in range(len(to))]
 
-    def spread(q):
-        far, home = role["far"][q:q + 1], role["home"]
-        off = engines(far)
-        on = [b for b in engines(home) if b not in off]
+    def fused(parts, dst_of, src_of, sem):
+        es = split(core, parts)
         g.remote_dma_fused([
-            RemoteDMATransfer(dst_ids=[did(d) for d in far], dma_engine_mask=bits(off), remote_sem=S.pcs,
-                              srcs=[piece(q)], dsts=[piece(q) for d in far], alu_op=0),
-            RemoteDMATransfer(dst_ids=[did(d) for d in home], dma_engine_mask=bits(on), remote_sem=S.rep,
-                              srcs=[piece(q)], dsts=[piece(q) for d in home], alu_op=0),
-        ], local_sem=S.snt)
-        cnt["snt"] += len(off) + len(on)
-        return len(off), len(on)
+            RemoteDMATransfer(dst_ids=[did(d) for d in part], dma_engine_mask=bits(es[b]), remote_sem=sem,
+                              srcs=[src_of(b)], dsts=[dst_of(b) for d in part], alu_op=0)
+            for b, part in enumerate(parts)], local_sem=S.snt)
+        cnt["snt"] += sum(len(e) for e in es)
+        return sum(len(e) for e in es)
 
-    kind = role["kind"]
-    is_rank = kind == "rank"
-    o = role["o"]
-    jobs = role["jobs"]
+    def part(o):
+        return T.tabs[128 * o:128 * (o + 1), :]
+
+    def cable():
+        fused([[role["relay"]]] * NB, lambda b: T.pcd[b], lambda b: T.pcd[b], S.pcs)
+
+    def spread(sem):
+        fused(role["to"], lambda b: part(role["o"]), lambda b: T.pcd[b], sem)
 
     def V(make):
         if cnt["vs"]:
@@ -161,155 +172,91 @@ def rank_program(g, core, T, topo):
         make().then_inc(S.vs, 1)
         cnt["vs"] += 1
 
-    def P(make):
-        make().then_inc(S.ts, 1)
-        cnt["ts"] += 1
-
-    if is_rank:
+    if kind == "rank":
         sy.dma_start(T.ptd[0:16, :], T.pt[:]).then_inc(S.ptc, 16)
         V(lambda: v.memset(T.zero[0:1, 0:224], 0))
         sc.wait_ge(S.vs, cnt["vs"])
         sc.dma_start(T.ptd[16:128, :], T.zero[0:1, 0:224]).then_inc(S.ptc, 16)
-        sc.dma_start(T.lcol[0:32, 2:3], T.pt[:]).then_inc(S.ldr, 16)
-        rows = (PG * 128) // NPC
-        for q in range(NPC):
-            (sy if q % 2 == 0 else sc).dma_start(piece(q), T.pool[rows * q:rows * (q + 1), :]).then_inc(S["tb%d" % q], 16)
-
-    V(lambda: v.memset(T.ones[0:32, 0:32], 1.0))
-    g.wait_ge(S.vs, cnt["vs"])
-    g.affine_select(T.U[0:32, 0:32], T.ones[0:32, 0:32], [[1, 32]], A.is_gt, 0.0, 0, -1).then_inc(S.gi, 1)
-    g.iota(T.iotaK[0:32, 0:128], [[1, CAPP], [0, SUB]], 0, 0, allow_small_or_imprecise_dtypes=True).then_inc(S.gi, 1)
-    g.iota(T.pidx[:, 0:1], [[1, 1]], 0, 1).then_inc(S.gi, 1)
-    ngi = 3
-    if is_rank:
-        g.iota(T.iotaO[0:32, 0:N], [[1, N]], 0, 0, allow_small_or_imprecise_dtypes=True).then_inc(S.gi, 1)
-        ngi = 4
-    v.wait_ge(S.gi, ngi)
-    te.wait_ge(S.gi, ngi)
-    V(lambda: v.tensor_scalar(T.pq[:, 0:1], T.pidx[:, 0:1], SUB - 1, None, A.bitwise_and))
-    V(lambda: v.tensor_copy(T.qc[:, 0:1], T.pq[:, 0:1]))
-
-    nrep = 0
-    if is_rank:
+        half = (PG * 128) // 2
+        sy.dma_start(T.P[0:64, :], T.pool[0:half, :]).then_inc(S.pl, 16)
+        sc.dma_start(T.P[64:128, :], T.pool[half:2 * half, :]).then_inc(S.pl, 16)
         g.wait_ge(S.ptc, 32)
-        srv = role["servers"]
-        eng = engines([d for d, _ in srv])
-        half = (len(srv) + 1) // 2
+        srv, slot = role["srv"], role["slot"]
+        eng = engines(core, srv)
+        h2 = len(srv) // 2
         g.remote_dma_fused([
-            RemoteDMATransfer(dst_ids=[did(d) for d, _ in part], dma_engine_mask=bits(eng[i:i + 1]), remote_sem=S.lq,
-                              srcs=[T.ptd[:]], dsts=[T.inbox[s] for _, s in part], alu_op=0)
-            for i, part in enumerate((srv[:half], srv[half:]))], local_sem=S.snt)
+            RemoteDMATransfer(dst_ids=[did(d) for d in pt_], dma_engine_mask=bits(eng[i:i + 1]), remote_sem=S.lq,
+                              srcs=[T.ptd[:]], dsts=[T.inbox[slot] for d in pt_], alu_op=0)
+            for i, pt_ in enumerate((srv[:h2], srv[h2:]))], local_sem=S.snt)
         cnt["snt"] += 2
-        hs = role["home"]
-        for q, h in enumerate(hs):
-            g.wait_ge(S["tb%d" % q], 16)
-            send(piece(q), piece(q), h, S.pcs, engines([h]))
-        g.wait_ge(S["tb%d" % (NPC - 1)], 16)
-        spread(NPC - 1)
-        for th in range(2):
-            g.iota(T.J[0:32, 256 * th:256 * (th + 1)], [[16, 2], [2, 8], [0, SUB]], th, -1,
-                   allow_small_or_imprecise_dtypes=True).then_inc(S.gj, 1)
-
-        v.wait_ge(S.ldr, 16)
-        V(lambda: v.tensor_scalar(T.ownr[0:32, 0:1], T.lcol[0:32, 2:3], 5, None, A.logical_shift_right))
-        V(lambda: v.tensor_copy(T.ownf[0:32, 0:1], T.ownr[0:32, 0:1]))
-        V(lambda: v.tensor_scalar(T.OH[0:32, 0:N], T.iotaO[0:32, 0:N], T.ownf[0:32, 0:1], None, A.is_equal))
-        te.wait_ge(S.vs, cnt["vs"])
-        P(lambda: te.matmul(T.pc[0:32, 0:N], T.U[0:32, 0:32], T.OH[0:32, 0:N], True, True))
-        V(lambda: v.tensor_scalar(T.own128[0:32, 0:1], T.ownf[0:32, 0:1], float(BLK), None, A.mult))
-        v.wait_ge(S.ts, cnt["ts"])
-        V(lambda: v.tensor_tensor(T.Pm[0:32, 0:N], T.pc[0:32, 0:N], T.OH[0:32, 0:N], A.mult))
-        V(lambda: v.tensor_reduce(T.kk[0:32, 0:1], T.Pm[0:32, 0:N], AxisListType.X, A.add))
-        V(lambda: v.tensor_scalar(T.sv[0:32, 0:1], T.kk[0:32, 0:1], float(SUB), T.own128[0:32, 0:1], A.mult, A.add))
-    elif kind == "home":
-        g.wait_ge(S.pcs, len(engines([cores[o]])))
-        noff, non = spread(role["q"])
-        nrep = non * (NPC - 1)
-    else:
-        g.wait_ge(S.pcs, len(engines([cores[o]])))
-        peers, q = role["peers"], role["q"]
-        eng = engines(peers)
-        g.remote_dma_fused([
-            RemoteDMATransfer(dst_ids=[did(d) for d in peers], dma_engine_mask=bits(eng), remote_sem=S.rep,
-                              srcs=[piece(q)], dsts=[piece(q) for d in peers], alu_op=0)], local_sem=S.snt)
-        cnt["snt"] += len(eng)
-        nrep = len(eng) * len(peers)
-
-    def group(pairs_sc, pk, pi):
-        c0, c1 = pairs_sc[0][1], pairs_sc[-1][1] + 1
-        V(lambda: v.tensor_scalar(T.own[0:32, c0:c1], T.lcol[0:32, c0:c1], 5, None, A.logical_shift_right))
-        V(lambda: v.tensor_scalar(T.vv[0:32, c0:c1], T.lcol[0:32, c0:c1], float(PG * o), float(SUB), A.subtract, A.mult))
-        V(lambda: v.tensor_scalar(T.e[0:32, c0:c1], T.own[0:32, c0:c1], float(o), None, A.is_equal))
-        te.wait_ge(S.vs, cnt["vs"])
-        P(lambda: te.matmul(pk[0:32, c0:c1], T.U[0:32, 0:32], T.e[0:32, c0:c1], True, True))
-        V(lambda: v.tensor_tensor(T.w[0:32, c0:c1], T.vv[0:32, c0:c1], T.e[0:32, c0:c1], A.mult))
-        v.wait_ge(S.ts, cnt["ts"])
-        for s, c in pairs_sc:
-            V(lambda: v.tensor_scalar(T.A[0:32, 128 * s:128 * (s + 1)], T.iotaK[0:32, 0:128], pk[0:32, c:c + 1], None, A.is_equal))
-        te.wait_ge(S.vs, cnt["vs"])
-        for s, c in pairs_sc:
-            P(lambda: te.matmul(pi[:, c:c + 1], T.A[0:32, 128 * s:128 * (s + 1)], T.w[0:32, c:c + 1], True, True))
-        v.wait_ge(S.ts, cnt["ts"])
-        V(lambda: v.tensor_scalar(T.idx[:, c0:c1], pi[:, c0:c1], T.qc[:, 0:1], None, A.add))
-        return cnt["vs"]
-
-    def gather(s, c):
-        g.indirect_dma_start(T.sb[:, RW * s:RW * (s + 1)], None, T.tab[:],
-                             IndirectOffsetOnAxis(ap=T.idx[:, c:c + 1], axis=0),
-                             bounds_check=PG * SUB - 1).then_inc(S["gs%d" % s], 16)
-
-    def reply(s):
-        g.wait_ge(S["gs%d" % s], 16)
-        send(T.land[BLK * o:BLK * (o + 1), :], T.sb[:, RW * s:RW * (s + 1)], cores[jobs[s]], S.arr, role["reng"])
-
-    nj = len(jobs)
-    for s in range(nj):
-        q = sy if s % 2 == 0 else sc
-        q.wait_ge(S.lq, nj)
-        q.dma_start(T.lcol[0:32, s:s + 1], T.inbox[s, 0:16, :]).then_inc(S.ld, 16)
-    v.wait_ge(S.ld, 16 * nj)
-
-    if not is_rank:
-        n1 = group([(s, s) for s in range(nj)], T.pk, T.pi)
-        g.wait_ge(S.rep, nrep)
-        g.wait_ge(S.vs, n1)
-        for s in range(nj):
-            gather(s, s)
-        for s in range(nj):
-            reply(s)
+        q3 = role["q"]
+        for qu in (sy, sc):
+            qu.wait_ge(S.pl, 32)
+        for b in range(NB):
+            c0 = PW * q3 + BW * b
+            (sy if b % 2 == 0 else sc).dma_start(T.pcd[b], T.P[:, c0:c0 + BW]).then_inc(S.own, 16)
+        g.wait_ge(S.pl, 32)
+        for q, h in enumerate(role["hold"]):
+            fused([[h]] * NB, lambda b: T.pcd[b], lambda b: T.P[:, PW * q + BW * b:PW * q + BW * (b + 1)], S.pcs)
+        g.wait_ge(S.own, 16 * NB)
+        cable()
+        spread(S.tbn)
+        narr = sum(len(engines(d, [core])) for d in srv)
+        for i, qu in enumerate((sy, sc)):
+            qu.wait_ge(S.arr, narr)
+            qu.dma_start(T.y[half * i:half * (i + 1), :], T.fin[64 * i:64 * (i + 1), :]).then_inc(S.st, 16)
+        g.wait_ge(S.arr, narr)
+        g.wait_ge(S.st, 32)
         g.wait_ge(S.snt, cnt["snt"])
         return
 
-    n1 = group([(0, 0), (1, 1), (2, 2)], T.pk, T.pi)
-    v.wait_ge(S.gj, 2)
-    V(lambda: v.tensor_scalar(T.Sel[0:32, 0:512], T.J[0:32, 0:512], 0.0, None, A.is_equal))
+    if kind in ("hold", "relay"):
+        g.wait_ge(S.pcs, sum(len(e) for e in split(role["src"], [[core]] * NB)))
+        if kind == "hold":
+            cable()
+            spread(S.tbn)
+        else:
+            spread(S.tbf)
+        g.wait_ge(S.snt, cnt["snt"])
+        return
+
+    reqs, s = role["reqs"], role["s"]
+    nr = len(reqs)
+    g.iota(T.J[0:32, 0:128], [[1, 2], [2, 16], [0, QU]], 0, -1, allow_small_or_imprecise_dtypes=True).then_inc(S.gi, 1)
+    g.iota(T.pidx[:, 0:1], [[1, 1]], 0, 1).then_inc(S.gi, 1)
+    v.wait_ge(S.gi, 2)
+    V(lambda: v.tensor_scalar(T.Sel[0:32, 0:128], T.J[0:32, 0:128], 0.0, None, A.is_equal))
+    V(lambda: v.tensor_scalar(T.pq[:, 0:1], T.pidx[:, 0:1], QU - 1, None, A.bitwise_and))
+    V(lambda: v.tensor_copy(T.qc[:, 0:1], T.pq[:, 0:1]))
+    for r in range(nr):
+        qu = sy if r % 2 == 0 else sc
+        qu.wait_ge(S.lq, nr)
+        qu.dma_start(T.lcol[0:32, r:r + 1], T.inbox[r, 0:16, :]).then_inc(S.ld, 16)
+    v.wait_ge(S.ld, 16 * nr)
+    V(lambda: v.tensor_scalar(T.val[0:32, 0:nr], T.lcol[0:32, 0:nr], float(QU), None, A.mult))
     te.wait_ge(S.vs, cnt["vs"])
-    for t in range(4):
-        P(lambda: te.matmul(T.pf[:, t:t + 1], T.Sel[0:32, 128 * t:128 * (t + 1)], T.sv[0:32, 0:1], True, True))
-    v.wait_ge(S.ts, cnt["ts"])
-    V(lambda: v.tensor_scalar(T.fidx[:, 0:4], T.pf[:, 0:4], T.qc[:, 0:1], None, A.add))
-    n2 = cnt["vs"]
+    te.matmul(T.pf[:, 0:nr], T.Sel[0:32, 0:128], T.val[0:32, 0:nr], True, True).then_inc(S.ts, 1)
+    v.wait_ge(S.ts, 1)
+    V(lambda: v.tensor_scalar(T.idx[:, 0:nr], T.pf[:, 0:nr], T.qc[:, 0:1], None, A.add))
 
-    g.wait_ge(S.vs, n1)
-    gather(0, 0)
-    gather(1, 1)
-    gather(2, 2)
-    reply(0)
-    reply(1)
-    sy.wait_ge(S.gs2, 16)
-    sy.dma_start(T.land[BLK * o:BLK * (o + 1), :], T.sb[:, RW * 2:RW * 3]).then_inc(S.selfc, 16)
-
-    narr = sum(len(plan[d]["reng"]) for d, _ in role["servers"])
-    g.wait_ge(S.arr, narr)
-    g.wait_ge(S.selfc, 16)
-    g.wait_ge(S.vs, n2)
-    for t in range(4):
-        g.indirect_dma_start(T.fin[:, RW * t:RW * (t + 1)], None, T.land[:],
-                             IndirectOffsetOnAxis(ap=T.fidx[:, t:t + 1], axis=0),
-                             bounds_check=N * BLK - 1).then_inc(S["fg%d" % t], 16)
-    for t in range(4):
-        q = sy if t % 2 == 0 else sc
-        q.wait_ge(S["fg%d" % t], 16)
-        q.dma_start(T.y[1024 * t:1024 * (t + 1), :], T.fin[:, RW * t:RW * (t + 1)]).then_inc(S.st, 16)
-    g.wait_ge(S.st, 64)
+    if "twin" in role:
+        plan = _PLAN["p"]
+        for wave, sem, relayed in ((role["waves"][0], S.tbn, False), (role["waves"][1], S.tbf, True)):
+            n = 0
+            for c, ro in plan.items():
+                for b, pt_ in enumerate(ro.get("to", [])):
+                    if core in pt_ and (ro["kind"] == "relay") == relayed:
+                        n += len(split(c, ro["to"])[b])
+            g.wait_ge(sem, n)
+            fused([[role["twin"]]] * len(wave), lambda b: part(wave[b]), lambda b: part(wave[b]), S.tb)
+    else:
+        g.wait_ge(S.tb, sum(len(e) for w in role["waves"] for e in split(role["feeder"], [[core]] * len(w))))
+    g.wait_ge(S.vs, cnt["vs"])
+    for r in range(nr):
+        g.indirect_dma_start(T.sb[:, BW * r:BW * (r + 1)], None, T.tabs[:],
+                             IndirectOffsetOnAxis(ap=T.idx[:, r:r + 1], axis=0),
+                             bounds_check=N * PG * QU - 1).then_inc(S["gs%d" % r], 16)
+    for r in range(nr):
+        g.wait_ge(S["gs%d" % r], 16)
+        send(T.fin[:, BW * s:BW * (s + 1)], T.sb[:, BW * r:BW * (r + 1)], reqs[r], S.arr)
     g.wait_ge(S.snt, cnt["snt"])

@@ -9,7 +9,8 @@ PW = RW // NH
 NS = 16
 BW = RW // NS
 NB = NS // NH
-NR = 3
+NR = 2
+NG = 3
 
 SCRATCH = {
     "ptd": ("dram", [128, 2], "int32"),
@@ -30,7 +31,7 @@ SCRATCH = {
     "Sel": ("sbuf", [128, 128], "float32"),
     "pf": ("psum", [128, 512], "float32"),
 }
-SEMAPHORES = ["ptc", "pl", "own", "lq", "pcs", "tbn", "tbf", "tb", "ld", "vs", "ts", "gi", "gs0", "gs1", "gs2",
+SEMAPHORES = ["ptc", "pl", "own", "lq", "pcs", "tbn", "tbf", "tb", "ld", "vs", "ts", "gi", "gs0", "gs1",
               "arr", "snt", "st"]
 
 _PLAN = {}
@@ -78,9 +79,9 @@ def make_plan(cores, topo):
             d = dies[s // NB]
             i = seen.get(d, 0)
             seen[d] = i + 1
-            two = [x for x in cand if (topo.host(x), topo.chip(x)) == places[i] and topo.die(x) == d][:2]
-            first[k].append(two[0])
-            twin[k].append(two[1])
+            grp = [x for x in cand if (topo.host(x), topo.chip(x)) == places[i] and topo.die(x) == d][:NG]
+            first[k].append(grp[0])
+            twin[k].append(grp)
 
     def targets(c, q):
         return [[first[rk(c)][NB * q + b]] for b in range(NB)]
@@ -92,20 +93,22 @@ def make_plan(cores, topo):
         for q, c in enumerate(hold):
             roles[c] = {"kind": "rank" if c == R else "hold", "o": o, "q": q, "relay": far[q], "to": targets(c, q), "src": R}
         roles[R]["hold"] = hold[:-1]
-        hs = [h for h in hosts if topo.rack(h) == rk(R)]
-        roles[R]["srv"] = (first if topo.host(R) == hs[0] else twin)[rk(R)]
-        roles[R]["slot"] = [x for x in cores if topo.host(x) == topo.host(R)].index(R)
+        i = [x for x in cores if rk(x) == rk(R)].index(R)
+        roles[R]["srv"] = [grp[i // NR] for grp in twin[rk(R)]]
+        roles[R]["slot"] = i % NR
         for q, c in enumerate(rel):
             roles[c] = {"kind": "relay", "o": info[partner][0], "q": q, "to": targets(c, q), "src": info[partner][1][q]}
     for k in racks:
-        hs = [h for h in hosts if topo.rack(h) == k]
+        mine = [x for x in cores if rk(x) == k]
         near = [o for o, R in enumerate(cores) if rk(R) == k]
         farp = [o for o, R in enumerate(cores) if rk(R) != k]
         for s in range(NS):
-            roles[first[k][s]] = {"kind": "srv", "s": s, "reqs": [x for x in cores if topo.host(x) == hs[0]],
-                                  "twin": twin[k][s], "waves": [near, farp]}
-            roles[twin[k][s]] = {"kind": "srv", "s": s, "reqs": [x for x in cores if topo.host(x) == hs[1]],
-                                 "feeder": first[k][s], "waves": [near, farp]}
+            for i, c in enumerate(twin[k][s]):
+                roles[c] = {"kind": "srv", "s": s, "reqs": mine[NR * i:NR * (i + 1)], "waves": [near, farp]}
+                if i == 0:
+                    roles[c]["twin"] = twin[k][s][1:]
+                else:
+                    roles[c]["feeder"] = first[k][s]
     return roles
 
 
@@ -248,7 +251,7 @@ def rank_program(g, core, T, topo):
                     if core in pt_ and (ro["kind"] == "relay") == relayed:
                         n += len(split(c, ro["to"])[b])
             g.wait_ge(sem, n)
-            fused([[role["twin"]]] * len(wave), lambda b: part(wave[b]), lambda b: part(wave[b]), S.tb)
+            fused([role["twin"]] * len(wave), lambda b: part(wave[b]), lambda b: part(wave[b]), S.tb)
     else:
         g.wait_ge(S.tb, sum(len(e) for w in role["waves"] for e in split(role["feeder"], [[core]] * len(w))))
     g.wait_ge(S.vs, cnt["vs"])

@@ -17,6 +17,7 @@ SCRATCH = {
     "inbox": ("dram", [NR, 128, 2], "int32"),
     "tabs": ("dram", [N * PG * QU, BW], "bfloat16"),
     "pcd": ("dram", [NB, 128, BW], "bfloat16"),
+    "pcr": ("dram", [NB, 128, BW], "bfloat16"),
     "zero": ("sbuf", [128, 224], "int32"),
     "P": ("sbuf", [128, RW], "bfloat16"),
     "sb": ("sbuf", [128, NR * BW], "bfloat16"),
@@ -31,7 +32,7 @@ SCRATCH = {
     "Sel": ("sbuf", [128, 128], "float32"),
     "pf": ("psum", [128, 512], "float32"),
 }
-SEMAPHORES = ["ptc", "pl", "own", "lq", "pcs", "tbn", "tbf", "tb", "ld", "vs", "ts", "gi", "gs0", "gs1",
+SEMAPHORES = ["ptc", "pl", "own", "lh", "lq", "pcs", "pcx", "tbn", "tbf", "tb", "ld", "vs", "ts", "gi", "gs0", "gs1",
               "arr", "snt", "st"]
 
 _PLAN = {}
@@ -46,6 +47,13 @@ def _engines(m):
     return [b for b in range(m.bit_length()) if (m >> b) & 1]
 
 
+def _deal(eng, n):
+    w = 1
+    while 2 * w * n <= len(eng):
+        w *= 2
+    return [eng[w * b:w * (b + 1)] for b in range(n)]
+
+
 def make_plan(cores, topo):
     def rk(x):
         return topo.rack(topo.host(x))
@@ -57,14 +65,14 @@ def make_plan(cores, topo):
         others = [p for p in pairs if R not in p]
         others.sort(key=lambda p: topo.die(p[0]) == topo.die(R))
         partner = [x for x in cores if x != R and topo.chip(x) == topo.chip(R) and topo.may_write(R, x) and rk(x) != rk(R)][0]
-        mine = [x for p in pairs if R in p for x in p if x != R]
-        info[R] = (o, [p[0] for p in others] + [R], [p[1] for p in others] + mine, partner)
+        mate = [x for p in pairs if R in p for x in p if x != R][0]
+        info[R] = (o, [p[0] for p in others] + [R], partner, mate)
     hosts = sorted({topo.host(R) for R in cores})
     racks = sorted({topo.rack(h) for h in hosts})
     taken = {(topo.host(R), topo.chip(R)) for R in cores}
     dies = [topo.die(x) for x in info[cores[0]][1]]
     per_die = max(dies.count(d) for d in dies) * NB
-    first, twin = {}, {}
+    grp = {}
     for k in racks:
         R0 = [R for R in cores if rk(R) == k][0]
         cand = [x for x in range((max(hosts) + 1) * topo.CORES_PER_HOST)
@@ -74,41 +82,48 @@ def make_plan(cores, topo):
         for h in hs:
             places += [(h, c) for c in sorted({topo.chip(x) for x in cand if topo.host(x) == h})[:per_die // len(hs)]]
         seen = {}
-        first[k], twin[k] = [], []
+        grp[k] = []
         for s in range(NS):
             d = dies[s // NB]
             i = seen.get(d, 0)
             seen[d] = i + 1
-            grp = [x for x in cand if (topo.host(x), topo.chip(x)) == places[i] and topo.die(x) == d][:NG]
-            first[k].append(grp[0])
-            twin[k].append(grp)
+            grp[k].append([x for x in cand if (topo.host(x), topo.chip(x)) == places[i] and topo.die(x) == d][:NG])
 
-    def targets(c, q):
-        return [[first[rk(c)][NB * q + b]] for b in range(NB)]
+    def member(o):
+        return [x for x, R in enumerate(cores) if rk(R) == rk(cores[o])].index(o) % NG
+
+    def targets(k, q, o):
+        return [[grp[k][NB * q + b][member(o)]] for b in range(NB)]
 
     roles = {}
     for R in cores:
-        o, hold, rel, partner = info[R]
-        far = info[partner][2]
+        o, hold, partner, mate = info[R]
+        po, phold = info[partner][0], info[partner][1]
+        k = rk(R)
+        i = [x for x in cores if rk(x) == k].index(R)
         for q, c in enumerate(hold):
-            roles[c] = {"kind": "rank" if c == R else "hold", "o": o, "q": q, "relay": far[q], "to": targets(c, q), "src": R}
+            roles[c] = {"kind": "rank" if c == R else "hold", "o": o, "q": q, "peer": phold[q], "src": R,
+                        "to": targets(k, q, o), "po": po, "fto": targets(k, q, po)}
+        for q, c in enumerate(hold[:-1] + [mate]):
+            if c == mate:
+                roles[c] = {"kind": "clerk"}
+            roles[c]["lsrv"] = [[grp[k][NB * q + b][i // NR]] for b in range(NB)]
+            roles[c]["slot"] = i % NR
         roles[R]["hold"] = hold[:-1]
-        i = [x for x in cores if rk(x) == rk(R)].index(R)
-        roles[R]["srv"] = [grp[i // NR] for grp in twin[rk(R)]]
-        roles[R]["slot"] = i % NR
-        for q, c in enumerate(rel):
-            roles[c] = {"kind": "relay", "o": info[partner][0], "q": q, "to": targets(c, q), "src": info[partner][1][q]}
+        roles[R]["clerks"] = hold[:-1] + [mate]
+        roles[R]["srv"] = [g_[i // NR] for g_ in grp[k]]
     for k in racks:
         mine = [x for x in cores if rk(x) == k]
         near = [o for o, R in enumerate(cores) if rk(R) == k]
         farp = [o for o, R in enumerate(cores) if rk(R) != k]
         for s in range(NS):
-            for i, c in enumerate(twin[k][s]):
-                roles[c] = {"kind": "srv", "s": s, "reqs": mine[NR * i:NR * (i + 1)], "waves": [near, farp]}
-                if i == 0:
-                    roles[c]["twin"] = twin[k][s][1:]
-                else:
-                    roles[c]["feeder"] = first[k][s]
+            q = s // NB
+            for i, c in enumerate(grp[k][s]):
+                nr_, fr_ = [o for o in near if member(o) == i], [o for o in farp if member(o) == i]
+                roles[c] = {"kind": "srv", "s": s, "reqs": mine[NR * i:NR * (i + 1)],
+                            "others": [x for x in grp[k][s] if x != c], "near": nr_, "far": fr_,
+                            "nfrom": [info[cores[o]][1][q] for o in nr_],
+                            "ffrom": [info[info[cores[o]][2]][1][q] for o in fr_]}
     return roles
 
 
@@ -124,11 +139,12 @@ def rank_program(g, core, T, topo):
     A = AluOpType
     kind = role["kind"]
 
-    def engines(src, dsts):
+    def engines(src, dsts, pick=None):
         m = -1
         for d in dsts:
             m &= topo.mask(src, d)
-        return _engines(m)
+        e = _engines(m)
+        return e if pick is None else e[pick::2]
 
     def bits(lst):
         return sum(1 << b for b in lst)
@@ -144,30 +160,29 @@ def rank_program(g, core, T, topo):
                      dma_engine_mask=bits(eng))
         cnt["snt"] += len(eng)
 
-    def split(src, to):
-        eng = engines(src, [d for part in to for d in part])
-        w = 1
-        while 2 * w * len(to) <= len(eng):
-            w *= 2
-        return [eng[w * b:w * (b + 1)] for b in range(len(to))]
+    def lanes(src, dst, n, pick=None):
+        return len(_deal(engines(src, [dst], pick), n)[0])
 
-    def fused(parts, dst_of, src_of, sem):
-        es = split(core, parts)
+    def fused(parts, dst_of, src_of, sem, pick=None):
+        es = _deal(engines(core, [d for part_ in parts for d in part_], pick), len(parts))
         g.remote_dma_fused([
-            RemoteDMATransfer(dst_ids=[did(d) for d in part], dma_engine_mask=bits(es[b]), remote_sem=sem,
-                              srcs=[src_of(b)], dsts=[dst_of(b) for d in part], alu_op=0)
-            for b, part in enumerate(parts)], local_sem=S.snt)
+            RemoteDMATransfer(dst_ids=[did(d) for d in part_], dma_engine_mask=bits(es[b]), remote_sem=sem,
+                              srcs=[src_of(b)], dsts=[dst_of(b) for d in part_], alu_op=0)
+            for b, part_ in enumerate(parts)], local_sem=S.snt)
         cnt["snt"] += sum(len(e) for e in es)
-        return sum(len(e) for e in es)
 
     def part(o):
         return T.tabs[128 * o:128 * (o + 1), :]
 
-    def cable():
-        fused([[role["relay"]]] * NB, lambda b: T.pcd[b], lambda b: T.pcd[b], S.pcs)
+    def pass_list():
+        g.wait_ge(S.lh, 1)
+        fused(role["lsrv"], lambda b: T.inbox[role["slot"]], lambda b: T.ptd[:], S.lq, 0)
 
-    def spread(sem):
-        fused(role["to"], lambda b: part(role["o"]), lambda b: T.pcd[b], sem)
+    def hold_and_relay():
+        fused([[role["peer"]]] * NB, lambda b: T.pcr[b], lambda b: T.pcd[b], S.pcx, 0)
+        fused(role["to"], lambda b: part(role["o"]), lambda b: T.pcd[b], S.tbn, 1)
+        g.wait_ge(S.pcx, NB * lanes(role["peer"], core, NB, 0))
+        fused(role["fto"], lambda b: part(role["po"]), lambda b: T.pcr[b], S.tbf)
 
     def V(make):
         if cnt["vs"]:
@@ -184,14 +199,11 @@ def rank_program(g, core, T, topo):
         sy.dma_start(T.P[0:64, :], T.pool[0:half, :]).then_inc(S.pl, 16)
         sc.dma_start(T.P[64:128, :], T.pool[half:2 * half, :]).then_inc(S.pl, 16)
         g.wait_ge(S.ptc, 32)
-        srv, slot = role["srv"], role["slot"]
-        eng = engines(core, srv)
-        h2 = len(srv) // 2
+        cl = role["clerks"]
         g.remote_dma_fused([
-            RemoteDMATransfer(dst_ids=[did(d) for d in pt_], dma_engine_mask=bits(eng[i:i + 1]), remote_sem=S.lq,
-                              srcs=[T.ptd[:]], dsts=[T.inbox[slot] for d in pt_], alu_op=0)
-            for i, pt_ in enumerate((srv[:h2], srv[h2:]))], local_sem=S.snt)
-        cnt["snt"] += 2
+            RemoteDMATransfer(dst_ids=[did(d) for d in cl], dma_engine_mask=bits(engines(core, cl)[0:1]), remote_sem=S.lh,
+                              srcs=[T.ptd[:]], dsts=[T.ptd[:] for d in cl], alu_op=0)], local_sem=S.snt)
+        cnt["snt"] += 1
         q3 = role["q"]
         for qu in (sy, sc):
             qu.wait_ge(S.pl, 32)
@@ -202,9 +214,8 @@ def rank_program(g, core, T, topo):
         for q, h in enumerate(role["hold"]):
             fused([[h]] * NB, lambda b: T.pcd[b], lambda b: T.P[:, PW * q + BW * b:PW * q + BW * (b + 1)], S.pcs)
         g.wait_ge(S.own, 16 * NB)
-        cable()
-        spread(S.tbn)
-        narr = sum(len(engines(d, [core])) for d in srv)
+        hold_and_relay()
+        narr = sum(len(engines(d, [core])) for d in role["srv"])
         for i, qu in enumerate((sy, sc)):
             qu.wait_ge(S.arr, narr)
             qu.dma_start(T.y[half * i:half * (i + 1), :], T.fin[64 * i:64 * (i + 1), :]).then_inc(S.st, 16)
@@ -213,13 +224,15 @@ def rank_program(g, core, T, topo):
         g.wait_ge(S.snt, cnt["snt"])
         return
 
-    if kind in ("hold", "relay"):
-        g.wait_ge(S.pcs, sum(len(e) for e in split(role["src"], [[core]] * NB)))
-        if kind == "hold":
-            cable()
-            spread(S.tbn)
-        else:
-            spread(S.tbf)
+    if kind == "clerk":
+        pass_list()
+        g.wait_ge(S.snt, cnt["snt"])
+        return
+
+    if kind == "hold":
+        pass_list()
+        g.wait_ge(S.pcs, NB * lanes(role["src"], core, NB))
+        hold_and_relay()
         g.wait_ge(S.snt, cnt["snt"])
         return
 
@@ -242,18 +255,12 @@ def rank_program(g, core, T, topo):
     v.wait_ge(S.ts, 1)
     V(lambda: v.tensor_scalar(T.idx[:, 0:nr], T.pf[:, 0:nr], T.qc[:, 0:1], None, A.add))
 
-    if "twin" in role:
-        plan = _PLAN["p"]
-        for wave, sem, relayed in ((role["waves"][0], S.tbn, False), (role["waves"][1], S.tbf, True)):
-            n = 0
-            for c, ro in plan.items():
-                for b, pt_ in enumerate(ro.get("to", [])):
-                    if core in pt_ and (ro["kind"] == "relay") == relayed:
-                        n += len(split(c, ro["to"])[b])
-            g.wait_ge(sem, n)
-            fused([role["twin"]] * len(wave), lambda b: part(wave[b]), lambda b: part(wave[b]), S.tb)
-    else:
-        g.wait_ge(S.tb, sum(len(e) for w in role["waves"] for e in split(role["feeder"], [[core]] * len(w))))
+    oth = role["others"]
+    for wave, frm, sem, pick in ((role["near"], role["nfrom"], S.tbn, 1), (role["far"], role["ffrom"], S.tbf, None)):
+        g.wait_ge(sem, sum(lanes(c, core, NB, pick) for c in frm))
+        fused([oth] * len(wave), lambda b: part(wave[b]), lambda b: part(wave[b]), S.tb)
+    plan = _PLAN["p"]
+    g.wait_ge(S.tb, sum(len(w) * lanes(c, core, len(w)) for c in oth for w in (plan[c]["near"], plan[c]["far"])))
     g.wait_ge(S.vs, cnt["vs"])
     for r in range(nr):
         g.indirect_dma_start(T.sb[:, BW * r:BW * (r + 1)], None, T.tabs[:],

@@ -6,11 +6,11 @@ QU = 4
 RW = 2048
 NH = 4
 PW = RW // NH
-NS = 16
+NS = 8
 BW = RW // NS
 NB = NS // NH
-NR = 2
-NG = 3
+NR = 1
+NG = 6
 
 SCRATCH = {
     "ptd": ("dram", [128, 2], "int32"),
@@ -32,7 +32,7 @@ SCRATCH = {
     "Sel": ("sbuf", [128, 128], "float32"),
     "pf": ("psum", [128, 512], "float32"),
 }
-SEMAPHORES = ["ptc", "pl", "own", "lh", "lq", "pcs", "pcx", "tbn", "tbf", "tb", "ld", "vs", "ts", "gi", "gs0", "gs1",
+SEMAPHORES = ["ptc", "pl", "own", "lh", "lq", "pcs", "pcx", "tbn", "tbf", "tb", "ld", "vs", "ts", "gi", "gs0",
               "arr", "snt", "st"]
 
 _PLAN = {}
@@ -58,21 +58,31 @@ def make_plan(cores, topo):
     def rk(x):
         return topo.rack(topo.host(x))
 
+    def tidx(R):
+        return [x for x in cores if rk(x) == rk(R)].index(R)
+
+    def cabled(R):
+        return [x for x in cores if x != R and topo.chip(x) == topo.chip(R) and topo.may_write(R, x) and rk(x) != rk(R)][0]
+
+    def turned(R):
+        return tidx(R if rk(R) == rk(cores[0]) else cabled(R)) % 2
+
     info = {}
     for o, R in enumerate(cores):
         cc = _chip_cores(R, topo)
         pairs = [cc[i:i + 2] for i in range(0, len(cc), 2)]
         others = [p for p in pairs if R not in p]
         others.sort(key=lambda p: topo.die(p[0]) == topo.die(R))
-        partner = [x for x in cores if x != R and topo.chip(x) == topo.chip(R) and topo.may_write(R, x) and rk(x) != rk(R)][0]
         mate = [x for p in pairs if R in p for x in p if x != R][0]
-        info[R] = (o, [p[0] for p in others] + [R], partner, mate)
+        hold = [p[0] for p in others] + [R]
+        if turned(R):
+            hold = hold[::-1]
+        j = len([x for x in cores[:o] if rk(x) == rk(R) and turned(x) == turned(R)])
+        info[R] = (o, hold, cabled(R), mate, tidx(R), j)
     hosts = sorted({topo.host(R) for R in cores})
     racks = sorted({topo.rack(h) for h in hosts})
     taken = {(topo.host(R), topo.chip(R)) for R in cores}
-    dies = [topo.die(x) for x in info[cores[0]][1]]
-    per_die = max(dies.count(d) for d in dies) * NB
-    grp = {}
+    on = {}
     for k in racks:
         R0 = [R for R in cores if rk(R) == k][0]
         cand = [x for x in range((max(hosts) + 1) * topo.CORES_PER_HOST)
@@ -80,50 +90,48 @@ def make_plan(cores, topo):
         hs = [h for h in hosts if topo.rack(h) == k]
         places = []
         for h in hs:
-            places += [(h, c) for c in sorted({topo.chip(x) for x in cand if topo.host(x) == h})[:per_die // len(hs)]]
-        seen = {}
-        grp[k] = []
+            places += [(h, c) for c in sorted({topo.chip(x) for x in cand if topo.host(x) == h})[:NS // len(hs)]]
+        on[k] = []
         for s in range(NS):
-            d = dies[s // NB]
-            i = seen.get(d, 0)
-            seen[d] = i + 1
-            grp[k].append([x for x in cand if (topo.host(x), topo.chip(x)) == places[i] and topo.die(x) == d][:NG])
+            here = [x for x in cand if (topo.host(x), topo.chip(x)) == places[s]]
+            on[k].append({d: [x for x in here if topo.die(x) == d][:NG // 2] for d in sorted({topo.die(x) for x in here})})
 
-    def member(o):
-        return [x for x, R in enumerate(cores) if rk(R) == rk(cores[o])].index(o) % NG
+    def group(k, s):
+        return [x for d in sorted(on[k][s]) for x in on[k][s][d]]
 
-    def targets(k, q, o):
-        return [[grp[k][NB * q + b][member(o)]] for b in range(NB)]
+    def taker(R, s):
+        return on[rk(R)][s][topo.die(info[R][1][s // NB])][info[R][5]]
+
+    def answers(R, s):
+        G = group(rk(R), s)
+        return G[(info[R][4] + (NG // 2) * (s % 2)) % NG]
 
     roles = {}
     for R in cores:
-        o, hold, partner, mate = info[R]
+        o, hold, partner, mate = info[R][:4]
         po, phold = info[partner][0], info[partner][1]
-        k = rk(R)
-        i = [x for x in cores if rk(x) == k].index(R)
         for q, c in enumerate(hold):
+            to = [[taker(R, NB * q + b)] for b in range(NB)]
             roles[c] = {"kind": "rank" if c == R else "hold", "o": o, "q": q, "peer": phold[q], "src": R,
-                        "to": targets(k, q, o), "po": po, "fto": targets(k, q, po)}
-        for q, c in enumerate(hold[:-1] + [mate]):
-            if c == mate:
-                roles[c] = {"kind": "clerk"}
-            roles[c]["lsrv"] = [[grp[k][NB * q + b][i // NR]] for b in range(NB)]
-            roles[c]["slot"] = i % NR
-        roles[R]["hold"] = hold[:-1]
-        roles[R]["clerks"] = hold[:-1] + [mate]
-        roles[R]["srv"] = [g_[i // NR] for g_ in grp[k]]
+                        "to": to, "po": po, "fto": to}
+        clerks = [mate if c == R else c for c in hold]
+        roles[mate] = {"kind": "clerk", "src": R}
+        for q, c in enumerate(clerks):
+            roles[c]["lsrv"] = [[answers(R, NB * q + b)] for b in range(NB)]
+            roles[c]["slot"] = 0
+        roles[R]["hold"] = sorted([(q, c) for q, c in enumerate(hold) if c != R],
+                                  key=lambda qc: topo.die(qc[1]) == topo.die(R))
+        roles[R]["clerks"] = clerks
+        roles[R]["srv"] = [answers(R, s) for s in range(NS)]
     for k in racks:
-        mine = [x for x in cores if rk(x) == k]
-        near = [o for o, R in enumerate(cores) if rk(R) == k]
-        farp = [o for o, R in enumerate(cores) if rk(R) != k]
         for s in range(NS):
-            q = s // NB
-            for i, c in enumerate(grp[k][s]):
-                nr_, fr_ = [o for o in near if member(o) == i], [o for o in farp if member(o) == i]
-                roles[c] = {"kind": "srv", "s": s, "reqs": mine[NR * i:NR * (i + 1)],
-                            "others": [x for x in grp[k][s] if x != c], "near": nr_, "far": fr_,
-                            "nfrom": [info[cores[o]][1][q] for o in nr_],
-                            "ffrom": [info[info[cores[o]][2]][1][q] for o in fr_]}
+            for c in group(k, s):
+                roles[c] = {"kind": "srv", "s": s, "others": [x for x in group(k, s) if x != c]}
+    for R in cores:
+        for s in range(NS):
+            h = info[R][1][s // NB]
+            roles[taker(R, s)].update({"near": [info[R][0]], "far": [info[info[R][2]][0]], "nfrom": [h], "ffrom": [h]})
+            roles[answers(R, s)].update({"reqs": [R], "lfrom": roles[R]["clerks"][s // NB]})
     return roles
 
 
@@ -211,7 +219,7 @@ def rank_program(g, core, T, topo):
             c0 = PW * q3 + BW * b
             (sy if b % 2 == 0 else sc).dma_start(T.pcd[b], T.P[:, c0:c0 + BW]).then_inc(S.own, 16)
         g.wait_ge(S.pl, 32)
-        for q, h in enumerate(role["hold"]):
+        for q, h in role["hold"]:
             fused([[h]] * NB, lambda b: T.pcd[b], lambda b: T.P[:, PW * q + BW * b:PW * q + BW * (b + 1)], S.pcs)
         g.wait_ge(S.own, 16 * NB)
         hold_and_relay()
@@ -246,7 +254,7 @@ def rank_program(g, core, T, topo):
     V(lambda: v.tensor_copy(T.qc[:, 0:1], T.pq[:, 0:1]))
     for r in range(nr):
         qu = sy if r % 2 == 0 else sc
-        qu.wait_ge(S.lq, nr)
+        qu.wait_ge(S.lq, nr * lanes(role["lfrom"], core, NB, 0))
         qu.dma_start(T.lcol[0:32, r:r + 1], T.inbox[r, 0:16, :]).then_inc(S.ld, 16)
     v.wait_ge(S.ld, 16 * nr)
     V(lambda: v.tensor_scalar(T.val[0:32, 0:nr], T.lcol[0:32, 0:nr], float(QU), None, A.mult))
@@ -256,11 +264,17 @@ def rank_program(g, core, T, topo):
     V(lambda: v.tensor_scalar(T.idx[:, 0:nr], T.pf[:, 0:nr], T.qc[:, 0:1], None, A.add))
 
     oth = role["others"]
+    sides = [[x for x in oth if topo.die(x) != topo.die(core)], [x for x in oth if topo.die(x) == topo.die(core)]]
     for wave, frm, sem, pick in ((role["near"], role["nfrom"], S.tbn, 1), (role["far"], role["ffrom"], S.tbf, None)):
         g.wait_ge(sem, sum(lanes(c, core, NB, pick) for c in frm))
-        fused([oth] * len(wave), lambda b: part(wave[b]), lambda b: part(wave[b]), S.tb)
+        for o in wave:
+            g.remote_dma_fused([
+                RemoteDMATransfer(dst_ids=[did(d) for d in side], dma_engine_mask=bits(engines(core, oth, i)), remote_sem=S.tb,
+                                  srcs=[part(o)], dsts=[part(o) for d in side], alu_op=0)
+                for i, side in enumerate(sides)], local_sem=S.snt)
+            cnt["snt"] += len(engines(core, oth))
     plan = _PLAN["p"]
-    g.wait_ge(S.tb, sum(len(w) * lanes(c, core, len(w)) for c in oth for w in (plan[c]["near"], plan[c]["far"])))
+    g.wait_ge(S.tb, sum(len(w) * len(engines(c, [core], 0)) for c in oth for w in (plan[c]["near"], plan[c]["far"])))
     g.wait_ge(S.vs, cnt["vs"])
     for r in range(nr):
         g.indirect_dma_start(T.sb[:, BW * r:BW * (r + 1)], None, T.tabs[:],

from concourse.bass import DstId, RemoteDMATransfer, IndirectOffsetOnAxis
from concourse.mybir import dt, AluOpType, AxisListType

N, PG, NP = 12, 32, 32
QU = 4
RW = 2048
NH = 4
PW = RW // NH
NS = 8
BW = RW // NS
NB = NS // NH
NR = 1
NG = 6

SCRATCH = {
    "ptd": ("dram", [128, 2], "int32"),
    "inbox": ("dram", [NR, 128, 2], "int32"),
    "tabs": ("dram", [N * PG * QU, BW], "bfloat16"),
    "pcd": ("dram", [NB, 128, BW], "bfloat16"),
    "pcr": ("dram", [NB, 128, BW], "bfloat16"),
    "zero": ("sbuf", [128, 224], "int32"),
    "P": ("sbuf", [128, RW], "bfloat16"),
    "sb": ("sbuf", [128, NR * BW], "bfloat16"),
    "fin": ("sbuf", [128, RW], "bfloat16"),
    "lcol": ("sbuf", [128, 4], "int32"),
    "val": ("sbuf", [128, 4], "float32"),
    "idx": ("sbuf", [128, 4], "int32"),
    "pidx": ("sbuf", [128, 4], "int32"),
    "pq": ("sbuf", [128, 4], "int32"),
    "qc": ("sbuf", [128, 4], "float32"),
    "J": ("sbuf", [128, 128], "float32"),
    "Sel": ("sbuf", [128, 128], "float32"),
    "pf": ("psum", [128, 512], "float32"),
}
SEMAPHORES = ["ptc", "pl", "own", "lh", "lq", "pcs", "pcx", "tbn", "tbf", "tb", "ld", "vs", "ts", "gi", "gs0",
              "arr", "snt", "st"]

_PLAN = {}


def _chip_cores(c, topo):
    n = topo.CORES_PER_CHIP
    return [x for x in range(max(0, c - n), c + n) if topo.host(x) == topo.host(c) and topo.chip(x) == topo.chip(c)]


def _engines(m):
    return [b for b in range(m.bit_length()) if (m >> b) & 1]


def _deal(eng, n):
    w = 1
    while 2 * w * n <= len(eng):
        w *= 2
    return [eng[w * b:w * (b + 1)] for b in range(n)]


def make_plan(cores, topo):
    def rk(x):
        return topo.rack(topo.host(x))

    def tidx(R):
        return [x for x in cores if rk(x) == rk(R)].index(R)

    def cabled(R):
        return [x for x in cores if x != R and topo.chip(x) == topo.chip(R) and topo.may_write(R, x) and rk(x) != rk(R)][0]

    def turned(R):
        return tidx(R if rk(R) == rk(cores[0]) else cabled(R)) % 2

    info = {}
    for o, R in enumerate(cores):
        cc = _chip_cores(R, topo)
        pairs = [cc[i:i + 2] for i in range(0, len(cc), 2)]
        others = [p for p in pairs if R not in p]
        others.sort(key=lambda p: topo.die(p[0]) == topo.die(R))
        mate = [x for p in pairs if R in p for x in p if x != R][0]
        hold = [p[0] for p in others] + [R]
        if turned(R):
            hold = hold[::-1]
        j = len([x for x in cores[:o] if rk(x) == rk(R) and turned(x) == turned(R)])
        info[R] = (o, hold, cabled(R), mate, tidx(R), j)
    hosts = sorted({topo.host(R) for R in cores})
    racks = sorted({topo.rack(h) for h in hosts})
    taken = {(topo.host(R), topo.chip(R)) for R in cores}
    on = {}
    for k in racks:
        R0 = [R for R in cores if rk(R) == k][0]
        cand = [x for x in range((max(hosts) + 1) * topo.CORES_PER_HOST)
                if topo.same_plane(x, R0) and (topo.host(x), topo.chip(x)) not in taken]
        hs = [h for h in hosts if topo.rack(h) == k]
        places = []
        for h in hs:
            places += [(h, c) for c in sorted({topo.chip(x) for x in cand if topo.host(x) == h})[:NS // len(hs)]]
        on[k] = []
        for s in range(NS):
            here = [x for x in cand if (topo.host(x), topo.chip(x)) == places[s]]
            on[k].append({d: [x for x in here if topo.die(x) == d][:NG // 2] for d in sorted({topo.die(x) for x in here})})

    def group(k, s):
        return [x for d in sorted(on[k][s]) for x in on[k][s][d]]

    def taker(R, s):
        return on[rk(R)][s][topo.die(info[R][1][s // NB])][info[R][5]]

    def answers(R, s):
        G = group(rk(R), s)
        return G[(info[R][4] + (NG // 2) * (s % 2)) % NG]

    roles = {}
    for R in cores:
        o, hold, partner, mate = info[R][:4]
        po, phold = info[partner][0], info[partner][1]
        for q, c in enumerate(hold):
            to = [[taker(R, NB * q + b)] for b in range(NB)]
            roles[c] = {"kind": "rank" if c == R else "hold", "o": o, "q": q, "peer": phold[q], "src": R,
                        "to": to, "po": po, "fto": to}
        clerks = [mate if c == R else c for c in hold]
        roles[mate] = {"kind": "clerk", "src": R}
        for q, c in enumerate(clerks):
            roles[c]["lsrv"] = [[answers(R, NB * q + b)] for b in range(NB)]
            roles[c]["slot"] = 0
        roles[R]["hold"] = sorted([(q, c) for q, c in enumerate(hold) if c != R],
                                  key=lambda qc: topo.die(qc[1]) == topo.die(R))
        roles[R]["clerks"] = clerks
        roles[R]["srv"] = [answers(R, s) for s in range(NS)]
    for k in racks:
        for s in range(NS):
            for c in group(k, s):
                roles[c] = {"kind": "srv", "s": s, "others": [x for x in group(k, s) if x != c]}
    for R in cores:
        for s in range(NS):
            h = info[R][1][s // NB]
            roles[taker(R, s)].update({"near": [info[R][0]], "far": [info[info[R][2]][0]], "nfrom": [h], "ffrom": [h]})
            roles[answers(R, s)].update({"reqs": [R], "lfrom": roles[R]["clerks"][s // NB]})
    return roles


def rank_program(g, core, T, topo):
    if "p" not in _PLAN:
        _PLAN["p"] = make_plan(list(T.cores), topo)
    role = _PLAN["p"].get(core)
    if role is None:
        return
    S = T.sem
    v, te, sy, sc = g.vector, g.tensor, g.sync, g.scalar
    cnt = {"vs": 0, "ts": 0, "snt": 0}
    A = AluOpType
    kind = role["kind"]

    def engines(src, dsts, pick=None):
        m = -1
        for d in dsts:
            m &= topo.mask(src, d)
        e = _engines(m)
        return e if pick is None else e[pick::2]

    def bits(lst):
        return sum(1 << b for b in lst)

    def did(d):
        rid, pid = topo.addr(d, core)
        return DstId(rid=rid, pnc=pid)

    def send(out_ap, in_ap, dst, sem):
        eng = engines(core, [dst])
        rid, pid = topo.addr(dst, core)
        g.remote_dma(out_ap=out_ap, in_ap=in_ap, remote_sem=sem, local_sem=S.snt, pid=pid, routing_id=rid,
                     dma_engine_mask=bits(eng))
        cnt["snt"] += len(eng)

    def lanes(src, dst, n, pick=None):
        return len(_deal(engines(src, [dst], pick), n)[0])

    def fused(parts, dst_of, src_of, sem, pick=None):
        es = _deal(engines(core, [d for part_ in parts for d in part_], pick), len(parts))
        g.remote_dma_fused([
            RemoteDMATransfer(dst_ids=[did(d) for d in part_], dma_engine_mask=bits(es[b]), remote_sem=sem,
                              srcs=[src_of(b)], dsts=[dst_of(b) for d in part_], alu_op=0)
            for b, part_ in enumerate(parts)], local_sem=S.snt)
        cnt["snt"] += sum(len(e) for e in es)

    def part(o):
        return T.tabs[128 * o:128 * (o + 1), :]

    def pass_list():
        g.wait_ge(S.lh, 1)
        fused(role["lsrv"], lambda b: T.inbox[role["slot"]], lambda b: T.ptd[:], S.lq, 0)

    def hold_and_relay():
        fused([[role["peer"]]] * NB, lambda b: T.pcr[b], lambda b: T.pcd[b], S.pcx, 0)
        fused(role["to"], lambda b: part(role["o"]), lambda b: T.pcd[b], S.tbn, 1)
        g.wait_ge(S.pcx, NB * lanes(role["peer"], core, NB, 0))
        fused(role["fto"], lambda b: part(role["po"]), lambda b: T.pcr[b], S.tbf)

    def V(make):
        if cnt["vs"]:
            v.wait_ge(S.vs, cnt["vs"])
        make().then_inc(S.vs, 1)
        cnt["vs"] += 1

    if kind == "rank":
        sy.dma_start(T.ptd[0:16, :], T.pt[:]).then_inc(S.ptc, 16)
        V(lambda: v.memset(T.zero[0:1, 0:224], 0))
        sc.wait_ge(S.vs, cnt["vs"])
        sc.dma_start(T.ptd[16:128, :], T.zero[0:1, 0:224]).then_inc(S.ptc, 16)
        half = (PG * 128) // 2
        sy.dma_start(T.P[0:64, :], T.pool[0:half, :]).then_inc(S.pl, 16)
        sc.dma_start(T.P[64:128, :], T.pool[half:2 * half, :]).then_inc(S.pl, 16)
        g.wait_ge(S.ptc, 32)
        cl = role["clerks"]
        g.remote_dma_fused([
            RemoteDMATransfer(dst_ids=[did(d) for d in cl], dma_engine_mask=bits(engines(core, cl)[0:1]), remote_sem=S.lh,
                              srcs=[T.ptd[:]], dsts=[T.ptd[:] for d in cl], alu_op=0)], local_sem=S.snt)
        cnt["snt"] += 1
        q3 = role["q"]
        for qu in (sy, sc):
            qu.wait_ge(S.pl, 32)
        for b in range(NB):
            c0 = PW * q3 + BW * b
            (sy if b % 2 == 0 else sc).dma_start(T.pcd[b], T.P[:, c0:c0 + BW]).then_inc(S.own, 16)
        g.wait_ge(S.pl, 32)
        for q, h in role["hold"]:
            fused([[h]] * NB, lambda b: T.pcd[b], lambda b: T.P[:, PW * q + BW * b:PW * q + BW * (b + 1)], S.pcs)
        g.wait_ge(S.own, 16 * NB)
        hold_and_relay()
        narr = sum(len(engines(d, [core])) for d in role["srv"])
        for i, qu in enumerate((sy, sc)):
            qu.wait_ge(S.arr, narr)
            qu.dma_start(T.y[half * i:half * (i + 1), :], T.fin[64 * i:64 * (i + 1), :]).then_inc(S.st, 16)
        g.wait_ge(S.arr, narr)
        g.wait_ge(S.st, 32)
        g.wait_ge(S.snt, cnt["snt"])
        return

    if kind == "clerk":
        pass_list()
        g.wait_ge(S.snt, cnt["snt"])
        return

    if kind == "hold":
        pass_list()
        g.wait_ge(S.pcs, NB * lanes(role["src"], core, NB))
        hold_and_relay()
        g.wait_ge(S.snt, cnt["snt"])
        return

    reqs, s = role["reqs"], role["s"]
    nr = len(reqs)
    g.iota(T.J[0:32, 0:128], [[1, 2], [2, 16], [0, QU]], 0, -1, allow_small_or_imprecise_dtypes=True).then_inc(S.gi, 1)
    g.iota(T.pidx[:, 0:1], [[1, 1]], 0, 1).then_inc(S.gi, 1)
    v.wait_ge(S.gi, 2)
    V(lambda: v.tensor_scalar(T.Sel[0:32, 0:128], T.J[0:32, 0:128], 0.0, None, A.is_equal))
    V(lambda: v.tensor_scalar(T.pq[:, 0:1], T.pidx[:, 0:1], QU - 1, None, A.bitwise_and))
    V(lambda: v.tensor_copy(T.qc[:, 0:1], T.pq[:, 0:1]))
    for r in range(nr):
        qu = sy if r % 2 == 0 else sc
        qu.wait_ge(S.lq, nr * lanes(role["lfrom"], core, NB, 0))
        qu.dma_start(T.lcol[0:32, r:r + 1], T.inbox[r, 0:16, :]).then_inc(S.ld, 16)
    v.wait_ge(S.ld, 16 * nr)
    V(lambda: v.tensor_scalar(T.val[0:32, 0:nr], T.lcol[0:32, 0:nr], float(QU), None, A.mult))
    te.wait_ge(S.vs, cnt["vs"])
    te.matmul(T.pf[:, 0:nr], T.Sel[0:32, 0:128], T.val[0:32, 0:nr], True, True).then_inc(S.ts, 1)
    v.wait_ge(S.ts, 1)
    V(lambda: v.tensor_scalar(T.idx[:, 0:nr], T.pf[:, 0:nr], T.qc[:, 0:1], None, A.add))

    oth = role["others"]
    sides = [[x for x in oth if topo.die(x) != topo.die(core)], [x for x in oth if topo.die(x) == topo.die(core)]]
    for wave, frm, sem, pick in ((role["near"], role["nfrom"], S.tbn, 1), (role["far"], role["ffrom"], S.tbf, None)):
        g.wait_ge(sem, sum(lanes(c, core, NB, pick) for c in frm))
        for o in wave:
            g.remote_dma_fused([
                RemoteDMATransfer(dst_ids=[did(d) for d in side], dma_engine_mask=bits(engines(core, oth, i)), remote_sem=S.tb,
                                  srcs=[part(o)], dsts=[part(o) for d in side], alu_op=0)
                for i, side in enumerate(sides)], local_sem=S.snt)
            cnt["snt"] += len(engines(core, oth))
    plan = _PLAN["p"]
    g.wait_ge(S.tb, sum(len(w) * len(engines(c, [core], 0)) for c in oth for w in (plan[c]["near"], plan[c]["far"])))
    g.wait_ge(S.vs, cnt["vs"])
    for r in range(nr):
        g.indirect_dma_start(T.sb[:, BW * r:BW * (r + 1)], None, T.tabs[:],
                             IndirectOffsetOnAxis(ap=T.idx[:, r:r + 1], axis=0),
                             bounds_check=N * PG * QU - 1).then_inc(S["gs%d" % r], 16)
    for r in range(nr):
        g.wait_ge(S["gs%d" % r], 16)
        send(T.fin[:, BW * s:BW * (s + 1)], T.sb[:, BW * r:BW * (r + 1)], reqs[r], S.arr)
    g.wait_ge(S.snt, cnt["snt"])
